import numpy as np
import ml_dtypes


def mxq(x, axis, fmt="e4m3"):
    dtype, down = {"e4m3": (ml_dtypes.float8_e4m3fn, 7), "e5m2": (ml_dtypes.float8_e5m2, 14)}[fmt]
    v = np.moveaxis(np.asarray(x, np.float32).astype(ml_dtypes.bfloat16).astype(np.float64), axis, -1)
    blocks = v.reshape(v.shape[:-1] + (-1, 32))
    amax = np.abs(blocks).max(-1, keepdims=True)
    byte = np.maximum(np.where(amax > 0, np.frexp(amax)[1] - 1 + 127, 0) - down, 1)
    scale = np.exp2(byte - 127.0)
    codes = (blocks / scale).astype(np.float32).astype(dtype).astype(np.float64)
    return np.moveaxis((codes * scale).reshape(v.shape), -1, axis)


WIDE = False


def mx_kscale(k):
    if not WIDE:
        return np.ones(k)
    levels = np.array([10, -10, 5, -5, 0])
    if k % 512:
        return np.exp2(np.random.permutation(np.resize(levels, k // 32))).repeat(32)
    a = np.empty((k // 512, 16))
    for p in range(k // 512):
        a[p, :8] = np.random.permutation(np.resize(levels, 8))
        for g in range(8):
            far = levels[np.abs(levels - a[p, g]) >= 10]
            a[p, g + 8] = far[np.random.randint(len(far))]
    return np.exp2(a.ravel()).repeat(32)


def f64(x):
    return np.asarray(x).astype(np.float64)


def striped(idx):
    return np.tile(idx.reshape(-1, 16).T, (8, 1)).astype(np.uint16)


def unstriped(offs):
    return offs[:16].T.reshape(-1).astype(np.int64)


E2M1 = np.array([0.0, 0.5, 1.0, 1.5, 2.0, 3.0, 4.0, 6.0, -0.0, -0.5, -1.0, -1.5, -2.0, -3.0, -4.0, -6.0])


def pack_weight(w, fmt):
    k, n = w.shape
    w = f64(np.asarray(w, np.float32).astype(ml_dtypes.bfloat16)).reshape(k // 32, 32, n)
    amax = np.abs(w).max(1)
    if fmt == "e4m3":
        byte = np.frexp(amax)[1] - 1 + 127 - 7
    else:
        mant, ex = np.frexp(amax / 6.0)
        byte = np.where(mant > 0.5, ex, ex - 1) + 127
    byte = np.clip(np.where(amax > 0, byte, 1), 1, 254)
    scaled = (w * np.exp2(127.0 - byte)[:, None, :]).reshape(k, n).astype(np.float32)
    by_word = np.ascontiguousarray(scaled.reshape(k // 512, 128, 4, n).transpose(0, 1, 3, 2))
    if fmt == "e4m3":
        words = by_word.astype(ml_dtypes.float8_e4m3fn).view(np.uint8)
    else:
        c = by_word.astype(ml_dtypes.float4_e2m1fn).view(np.uint8) & 0xF
        words = (c[..., 0::2] | (c[..., 1::2] << 4)).reshape(k // 512, 128, 2 * n)
    return np.ascontiguousarray(words), np.ascontiguousarray(byte.astype(np.uint8).reshape(k // 512, 16, n))


def unpack_weight(words, scales, fmt):
    g, _, n = scales.shape
    words = np.ascontiguousarray(words).reshape(g, 128, n, -1)
    if fmt == "e4m3":
        vals = words.view(ml_dtypes.float8_e4m3fn).astype(np.float64)
    else:
        nib = np.empty((g, 128, n, 4), np.uint8)
        nib[..., 0::2] = words & 0xF
        nib[..., 1::2] = words >> 4
        vals = E2M1[nib]
    vals = vals * np.repeat(np.exp2(scales.astype(np.float64) - 127.0), 8, axis=1)[..., None]
    return vals.transpose(0, 1, 3, 2).reshape(g * 512, n)


K, T, E1, C1, E2, C2, H = 512, 512, 4, 128, 4, 128, 512
N = 256


def deal(E, C):
    slot_token = np.random.permutation(T)
    return slot_token, None, np.random.uniform(0.2, 1.0, T)


def by_expert(wq, xq, E, C):
    return np.concatenate([wq[e].T @ xq[:, e * C:(e + 1) * C] for e in range(E)], axis=1)


def setup_inputs():
    n = np.random.standard_normal
    s = mx_kscale(K)
    u = mx_kscale(H)
    slots1, pos1, g1 = deal(E1, C1)
    slots2, pos2, g2 = deal(E2, C2)
    x = pack_weight(n((K, T)) * s[:, None], "e4m3")
    w1 = [pack_weight(m, "e2m1") for m in n((E1, K, H)) / np.sqrt(K) / s[None, :, None] * u]
    return {
        "x_words": x[0],
        "x_scales": x[1],
        "w1_words": np.stack([m[0] for m in w1]),
        "w1_scales": np.stack([m[1] for m in w1]),
        "w2": (n((E2, H, N)) / np.sqrt(H) / u[None, :, None]).astype(np.float32),
        "gate1": (np.tile(g1, (128, 1))).astype(np.float32),
        "gate2": (np.tile(g2, (128, 1))).astype(np.float32),
        "offs": striped(slots1),
        "offs2": striped(slots2),
    }


def reference(x_words, x_scales, w1_words, w1_scales, w2, gate1, gate2, offs, offs2):
    w1 = np.stack([unpack_weight(w1_words[e], w1_scales[e], "e2m1") for e in range(E1)])
    w2q = mxq(f64(w2), 1, "e4m3")
    idx, idx2 = unstriped(offs), unstriped(offs2)
    xq = unpack_weight(x_words, x_scales, "e4m3")[:, idx]
    h = by_expert(w1, xq, E1, C1)
    c = np.zeros((H, T))
    c[:, idx] = f64(gate1[:1]) * h
    y = by_expert(w2q, mxq(c[:, idx2], 0, "e4m3"), E2, C2)
    out = np.zeros((N, T))
    out[:, idx2] = f64(gate2[:1]) * y
    return out

@@ -1,0 +1,206 @@
+from contextlib import ExitStack
+
+import concourse.mybir as mybir
+from concourse.masks import make_identity
+
+F32 = mybir.dt.float32
+BF16 = mybir.dt.bfloat16
+I32 = mybir.dt.int32
+U32 = mybir.dt.uint32
+U16 = mybir.dt.uint16
+U8 = mybir.dt.uint8
+FP8X4 = mybir.dt.float8_e4m3fn_x4
+FP4X4 = mybir.dt.float4_e2m1fn_x4
+COPY = mybir.ActivationFunctionType.Copy
+
+P = 128
+T = 512
+H = 512
+N = 256
+E = 4
+C = 128
+LIST_COLS = C // 16
+
+FLOPS = 2 * T * 512 * H + 2 * T * H * N
+
+
+def tile_moe_ser_none_kernel(tc, x_words, x_scales, w1_words, w1_scales, w2, gate1, gate2, offs, offs2, out):
+    nc = tc.nc
+    with ExitStack() as ctx:
+        keep = ctx.enter_context(tc.tile_pool(name="keep", bufs=1))
+        psum = ctx.enter_context(tc.psum_pool(name="psum", bufs=8))
+
+        def slots(e):
+            return slice(e * C, (e + 1) * C)
+
+        def entries(e):
+            return slice(e * LIST_COLS, (e + 1) * LIST_COLS)
+
+        list1 = keep.tile([P, T // 16], U16, name="list1")
+        list2 = keep.tile([P, T // 16], U16, name="list2")
+        xw = keep.tile([P, T], I32, name="xw", align_bytes=64)
+        xs = keep.tile([P, T], U8, name="xs", align_bytes=64)
+        w1w = keep.tile([P, E, 2 * H], U8, name="w1w", align_bytes=64)
+        w1s = keep.tile([P, E, H], U8, name="w1s", align_bytes=64)
+        g1rows = keep.tile([P, C], F32, name="g1rows")
+        g2rows = keep.tile([P, C], F32, name="g2rows")
+        w2raw = [keep.tile([P, 4, N], F32, name="w2raw%d" % f) for f in range(E)]
+        ident = keep.tile([P, P], F32, name="ident")
+
+        nc.vector.memset(xs[:].bitcast(I32), 0)
+        nc.vector.memset(w1s[:].rearrange("p e n -> p (e n)").bitcast(I32), 0)
+
+        xs_rows = x_scales[0].rearrange("(q r) n -> r q n", r=4)
+        w1s_rows = w1_scales[:, 0].rearrange("e (q r) n -> r q e n", r=4)
+        nc.sync.dma_start(list1[:], offs)
+        nc.sync.dma_start(xw[:], x_words[0].rearrange("p t d -> p (t d)").bitcast(I32))
+        for r in range(4):
+            nc.sync.dma_start(xs[r:P:32, :].bitcast(I32), xs_rows[r].bitcast(I32))
+        for r in range(4):
+            queue = nc.sync if r < 2 else nc.gpsimd
+            queue.dma_start(w1s[r:P:32, :, :].bitcast(I32), w1s_rows[r].bitcast(I32))
+        make_identity(nc, ident[:])
+        nc.sync.dma_start(w1w[:, 0, :].bitcast(I32), w1_words[0, 0].bitcast(I32))
+        nc.sync.dma_start(g1rows[:], gate1[0:32, :].rearrange("r (e c) -> (r e) c", c=C))
+        nc.sync.dma_start(w1w[:, 1, :].bitcast(I32), w1_words[1, 0].bitcast(I32))
+        nc.sync.dma_start(w1w[:, 2:4, :].bitcast(I32), w1_words[2:4, 0].rearrange("e p n -> p e n").bitcast(I32))
+        for f in range(E):
+            nc.sync.dma_start(w2raw[f][:], w2[f].rearrange("(p j) n -> p j n", j=4))
+            if f == 0:
+                nc.sync.dma_start(list2[:], offs2)
+                nc.sync.dma_start(g2rows[:], gate2[0:32, :].rearrange("r (e c) -> (r e) c", c=C))
+
+        def gate_columns(rows, name):
+            bank = psum.tile([P, 512], F32, name="bank", tag="bank")
+            nc.tensor.transpose(bank[:, 0:P], rows[:], ident[:])
+            cols = keep.tile([P, E], F32, name=name)
+            nc.scalar.copy(cols[:], bank[:, 0:E])
+            return cols
+
+        g1 = gate_columns(g1rows, "g1")
+
+        xgw = keep.tile([P, T], U32, name="xgw", align_bytes=64)
+        xgs = keep.tile([P, T], U8, name="xgs", align_bytes=64)
+        hrow = [keep.tile([P, 4, P], F32, name="hrow%d" % e, align_bytes=64) for e in range(E)]
+        hcol = keep.tile([P, 4, T], F32, name="hcol", align_bytes=64)
+        ctok = [keep.tile([P, T], F32, name="ctok%d" % t, align_bytes=64) for t in range(4)]
+        cpair = [keep.tile([P, T, 2], BF16, name="cpair%d" % u, align_bytes=64) for u in range(2)]
+
+        def layer1_product(e):
+            nc.vector.tensor_copy(xgw[:, slots(e)], xw[:].bitcast(U32).indirect(list1[:, entries(e)]))
+            nc.vector.tensor_copy(xgs[:, slots(e)], xs[:].indirect(list1[:, entries(e)]))
+            bank = psum.tile([P, 512], F32, name="bank", tag="bank")
+            nc.tensor.matmul_mx(
+                out=bank[:],
+                lhsT=xgw[:, slots(e)].bitcast(FP8X4),
+                lhsT_scale=xgs[:, slots(e)],
+                rhs=w1w[:, e, :].bitcast(FP4X4),
+                rhs_scale=w1s[:, e, :],
+                start=True,
+                stop=True,
+            )
+            nc.scalar.activation(
+                out=hrow[e][:],
+                in_=bank[:].rearrange("s (p t) -> s t p", t=4),
+                func=COPY,
+                scale=g1[:, e : e + 1],
+            )
+
+        def layer1_turn(e):
+            bank = psum.tile([P, 512], F32, name="bank", tag="bank")
+            for t in range(4):
+                nc.tensor.transpose(bank[:, t * C : (t + 1) * C], hrow[e][:, t, :], ident[:])
+            nc.scalar.copy(hcol[:, :, slots(e)], bank[:].rearrange("p (t s) -> p t s", t=4))
+
+        def layer1_scatter(t, first, last):
+            nc.vector.tensor_copy(
+                ctok[t][:].indirect(list1[:, first * LIST_COLS : (last + 1) * LIST_COLS]),
+                hcol[:, t, first * C : (last + 1) * C],
+            )
+
+        def pair_up(t):
+            nc.scalar.copy(cpair[t // 2][:, :, t % 2], ctok[t][:])
+
+        w2b = [keep.tile([P, N, 4], BF16, name="w2b%d" % f, align_bytes=64) for f in range(E)]
+        w2w = keep.tile([P, E, N], U32, name="w2w", align_bytes=64)
+        w2s = keep.tile([P, E, N], U8, name="w2s", align_bytes=64)
+
+        def w2_round(f):
+            nc.scalar.copy(
+                w2b[f][:].rearrange("p (c i) t -> p c t i", i=4),
+                w2raw[f][:].rearrange("p t (c i) -> p c t i", i=4),
+            )
+
+        def w2_quantise(f):
+            nc.vector.quantize_mx(
+                out=w2w[:, f, :].bitcast(FP8X4),
+                scales=w2s[:, f, :],
+                in_=w2b[f][:].rearrange("p n t -> p (n t)"),
+            )
+
+        layer1_product(0)
+        for e in range(1, E):
+            layer1_product(e)
+            layer1_turn(e - 1)
+        layer1_turn(E - 1)
+        g2 = gate_columns(g2rows, "g2")
+        for t in range(4):
+            layer1_scatter(t, 0, 0)
+        for e in range(1, E):
+            for t in range(2):
+                layer1_scatter(t, e, e)
+        w2_round(0)
+        pair_up(0)
+        pair_up(1)
+        for t in range(2, 4):
+            layer1_scatter(t, 1, E - 1)
+            pair_up(t)
+
+        cg = keep.tile([P, T, 2], U32, name="cg", align_bytes=64)
+        cw = keep.tile([P, T], U32, name="cw", align_bytes=64)
+        cs = keep.tile([P, T], U8, name="cs", align_bytes=64)
+        yrow = [keep.tile([P, N], F32, name="yrow%d" % f, align_bytes=64) for f in range(E)]
+        ycol = keep.tile([P, 2, T], F32, name="ycol", align_bytes=64)
+        otok = [keep.tile([P, T], F32, name="otok%d" % v, align_bytes=64) for v in range(2)]
+
+        def layer2_gather(f, u):
+            nc.vector.tensor_copy(cg[:, slots(f), u], cpair[u][:].rearrange("p s d -> p (s d)").bitcast(U32).indirect(list2[:, entries(f)]))
+
+        def layer2_product(f):
+            nc.vector.quantize_mx(
+                out=cw[:, slots(f)].bitcast(FP8X4),
+                scales=cs[:, slots(f)],
+                in_=cg[:, slots(f), :].rearrange("p s u -> p (s u)").bitcast(BF16),
+            )
+            bank = psum.tile([P, 512], F32, name="bank", tag="bank")
+            nc.tensor.matmul_mx(
+                out=bank[:, 0:N],
+                lhsT=cw[:, slots(f)].bitcast(FP8X4),
+                lhsT_scale=cs[:, slots(f)],
+                rhs=w2w[:, f, :].bitcast(FP8X4),
+                rhs_scale=w2s[:, f, :],
+                start=True,
+                stop=True,
+            )
+            nc.scalar.activation(out=yrow[f][:], in_=bank[:, 0:N], func=COPY, scale=g2[:, f : f + 1])
+
+        def layer2_turn(f):
+            bank = psum.tile([P, 512], F32, name="bank", tag="bank")
+            for v in range(2):
+                nc.tensor.transpose(bank[:, v * C : (v + 1) * C], yrow[f][:, v * P : (v + 1) * P], ident[:])
+            nc.scalar.copy(ycol[:, :, slots(f)], bank[:, 0 : 2 * C].rearrange("p (v s) -> p v s", v=2))
+
+        for f in range(1, E):
+            w2_round(f)
+        for f in range(E):
+            layer2_gather(f, 0)
+        for f in range(E):
+            layer2_gather(f, 1)
+            w2_quantise(f)
+            layer2_product(f)
+            layer2_turn(f)
+        for f in range(E):
+            for v in range(2):
+                nc.vector.tensor_copy(otok[v][:].indirect(list2[:, entries(f)]), ycol[:, v, slots(f)])
+        for v in range(2):
+            nc.sync.dma_start(out[v * P : (v + 1) * P, :], otok[v][:])

@@ -20,6 +20,7 @@ N = 256
 E = 4
 C = 128
 LIST_COLS = C // 16
+WIDE = 704
 
 FLOPS = 2 * T * 512 * H + 2 * T * H * N
 
@@ -40,35 +41,30 @@ def tile_moe_ser_none_kernel(tc, x_words, x_scales, w1_words, w1_scales, w2, gat
         list2 = keep.tile([P, T // 16], U16, name="list2")
         xw = keep.tile([P, T], I32, name="xw", align_bytes=64)
         xs = keep.tile([P, T], U8, name="xs", align_bytes=64)
-        w1w = keep.tile([P, E, 2 * H], U8, name="w1w", align_bytes=64)
+        w1first = keep.tile([P, 2 * H], U8, name="w1first", align_bytes=64)
         w1s = keep.tile([P, E, H], U8, name="w1s", align_bytes=64)
-        g1rows = keep.tile([P, C], F32, name="g1rows")
-        g2rows = keep.tile([P, C], F32, name="g2rows")
-        w2raw = [keep.tile([P, 4, N], F32, name="w2raw%d" % f) for f in range(E)]
+        g1rows = keep.tile([P, C], F32, name="g1rows", tag="late", align_bytes=64)
         ident = keep.tile([P, P], F32, name="ident")
 
-        nc.vector.memset(xs[:].bitcast(I32), 0)
+        nc.gpsimd.memset(xs[:].bitcast(I32), 0)
         nc.vector.memset(w1s[:].rearrange("p e n -> p (e n)").bitcast(I32), 0)
 
         xs_rows = x_scales[0].rearrange("(q r) n -> r q n", r=4)
         w1s_rows = w1_scales[:, 0].rearrange("e (q r) n -> r q e n", r=4)
+        make_identity(nc, ident[:])
         nc.sync.dma_start(list1[:], offs)
         nc.sync.dma_start(xw[:], x_words[0].rearrange("p t d -> p (t d)").bitcast(I32))
         for r in range(4):
-            nc.sync.dma_start(xs[r:P:32, :].bitcast(I32), xs_rows[r].bitcast(I32))
-        for r in range(4):
-            queue = nc.sync if r < 2 else nc.gpsimd
-            queue.dma_start(w1s[r:P:32, :, :].bitcast(I32), w1s_rows[r].bitcast(I32))
-        make_identity(nc, ident[:])
-        nc.sync.dma_start(w1w[:, 0, :].bitcast(I32), w1_words[0, 0].bitcast(I32))
+            nc.scalar.dma_start(xs[r:P:32, :].bitcast(I32), xs_rows[r].bitcast(I32))
         nc.sync.dma_start(g1rows[:], gate1[0:32, :].rearrange("r (e c) -> (r e) c", c=C))
-        nc.sync.dma_start(w1w[:, 1, :].bitcast(I32), w1_words[1, 0].bitcast(I32))
-        nc.sync.dma_start(w1w[:, 2:4, :].bitcast(I32), w1_words[2:4, 0].rearrange("e p n -> p e n").bitcast(I32))
-        for f in range(E):
-            nc.sync.dma_start(w2raw[f][:], w2[f].rearrange("(p j) n -> p j n", j=4))
-            if f == 0:
-                nc.sync.dma_start(list2[:], offs2)
-                nc.sync.dma_start(g2rows[:], gate2[0:32, :].rearrange("r (e c) -> (r e) c", c=C))
+        nc.sync.dma_start(w1first[:].bitcast(I32), w1_words[0, 0].bitcast(I32))
+        for r in range(4):
+            nc.sync.dma_start(w1s[r:P:32, :, :].bitcast(I32), w1s_rows[r].bitcast(I32))
+        w1rest = keep.tile([P, E - 1, 2 * H], U8, name="w1rest", align_bytes=64)
+        nc.sync.dma_start(w1rest[:, 0, :].bitcast(I32), w1_words[1, 0].bitcast(I32))
+        nc.sync.dma_start(w1rest[:, 1:3, :].bitcast(I32), w1_words[2:4, 0].rearrange("e p n -> p e n").bitcast(I32))
+        w1w = [w1first[:]] + [w1rest[:, e, :] for e in range(E - 1)]
+        nc.sync.dma_start(list2[:], offs2)
 
         def gate_columns(rows, name):
             bank = psum.tile([P, 512], F32, name="bank", tag="bank")
@@ -79,12 +75,20 @@ def tile_moe_ser_none_kernel(tc, x_words, x_scales, w1_words, w1_scales, w2, gat
 
         g1 = gate_columns(g1rows, "g1")
 
+        late = keep.tile([P, E * 4 * N + T], F32, name="late", tag="late", align_bytes=64)
+        w2raw = [late[:, f * 4 * N : (f + 1) * 4 * N].rearrange("p (j n) -> p j n", j=4) for f in range(E)]
+        g2 = late[:, E * 4 * N : E * 4 * N + T]
+        for f in range(E):
+            nc.sync.dma_start(w2raw[f], w2[f].rearrange("(p j) n -> p j n", j=4))
+        nc.sync.dma_start(g2, gate2)
+
         xgw = keep.tile([P, T], U32, name="xgw", align_bytes=64)
         xgs = keep.tile([P, T], U8, name="xgs", align_bytes=64)
-        hrow = [keep.tile([P, 4, P], F32, name="hrow%d" % e, align_bytes=64) for e in range(E)]
+        hrow = [keep.tile([P, 2, P, 2], BF16, name="hrow%d" % e, tag="hrow%d" % e, align_bytes=64) for e in range(E)]
         hcol = keep.tile([P, 4, T], F32, name="hcol", align_bytes=64)
-        ctok = [keep.tile([P, T], F32, name="ctok%d" % t, align_bytes=64) for t in range(4)]
-        cpair = [keep.tile([P, T, 2], BF16, name="cpair%d" % u, align_bytes=64) for u in range(2)]
+        ctok = [keep.tile([P, T if t < 2 else WIDE], F32, name="ctok%d" % t, align_bytes=64) for t in range(4)]
+        cround = [keep.tile([P, T], BF16, name="cround%d" % t, align_bytes=64) for t in range(4)]
+        cg = keep.tile([P, T, 4], BF16, name="cg", align_bytes=64)
 
         def layer1_product(e):
             nc.vector.tensor_copy(xgw[:, slots(e)], xw[:].bitcast(U32).indirect(list1[:, entries(e)]))
@@ -94,23 +98,31 @@ def tile_moe_ser_none_kernel(tc, x_words, x_scales, w1_words, w1_scales, w2, gat
                 out=bank[:],
                 lhsT=xgw[:, slots(e)].bitcast(FP8X4),
                 lhsT_scale=xgs[:, slots(e)],
-                rhs=w1w[:, e, :].bitcast(FP4X4),
+                rhs=w1w[e].bitcast(FP4X4),
                 rhs_scale=w1s[:, e, :],
                 start=True,
                 stop=True,
             )
             nc.scalar.activation(
                 out=hrow[e][:],
-                in_=bank[:].rearrange("s (p t) -> s t p", t=4),
+                in_=bank[:].rearrange("s (p u d) -> s u p d", u=2, d=2),
                 func=COPY,
                 scale=g1[:, e : e + 1],
             )
 
+        turned = []
+
         def layer1_turn(e):
             bank = psum.tile([P, 512], F32, name="bank", tag="bank")
-            for t in range(4):
-                nc.tensor.transpose(bank[:, t * C : (t + 1) * C], hrow[e][:, t, :], ident[:])
-            nc.scalar.copy(hcol[:, :, slots(e)], bank[:].rearrange("p (t s) -> p t s", t=4))
+            words = hrow[e][:].rearrange("s u p d -> s (u p d)").bitcast(F32)
+            for u in range(2):
+                nc.tensor.transpose(bank[:, u * C : (u + 1) * C], words[:, u * P : (u + 1) * P], ident[:])
+            turned.append(bank)
+            layer1_planes(e, 0)
+
+        def layer1_planes(e, u):
+            pairs = turned[e][:, u * C : (u + 1) * C].bitcast(BF16).rearrange("p (s d) -> p d s", d=2)
+            nc.scalar.copy(hcol[:, 2 * u : 2 * u + 2, slots(e)], pairs)
 
         def layer1_scatter(t, first, last):
             nc.vector.tensor_copy(
@@ -118,24 +130,29 @@ def tile_moe_ser_none_kernel(tc, x_words, x_scales, w1_words, w1_scales, w2, gat
                 hcol[:, t, first * C : (last + 1) * C],
             )
 
-        def pair_up(t):
-            nc.scalar.copy(cpair[t // 2][:, :, t % 2], ctok[t][:])
+        def layer2_gather(t, first, last):
+            nc.scalar.activation(
+                out=cg[:, first * C : (last + 1) * C, t],
+                in_=cround[t][:].indirect(list2[:, first * LIST_COLS : (last + 1) * LIST_COLS]),
+                func=COPY,
+            )
 
-        w2b = [keep.tile([P, N, 4], BF16, name="w2b%d" % f, align_bytes=64) for f in range(E)]
+        w2b = [keep.tile([P, N, 4], BF16, name="w2b0", align_bytes=64)[:]]
         w2w = keep.tile([P, E, N], U32, name="w2w", align_bytes=64)
         w2s = keep.tile([P, E, N], U8, name="w2s", align_bytes=64)
 
         def w2_round(f):
-            nc.scalar.copy(
-                w2b[f][:].rearrange("p (c i) t -> p c t i", i=4),
-                w2raw[f][:].rearrange("p t (c i) -> p c t i", i=4),
+            copy = nc.vector.tensor_copy if f == 0 else nc.scalar.copy
+            copy(
+                w2b[f].rearrange("p (c i) t -> p c t i", i=4),
+                w2raw[f].rearrange("p t (c i) -> p c t i", i=4),
             )
 
         def w2_quantise(f):
             nc.vector.quantize_mx(
                 out=w2w[:, f, :].bitcast(FP8X4),
                 scales=w2s[:, f, :],
-                in_=w2b[f][:].rearrange("p n t -> p (n t)"),
+                in_=w2b[f].rearrange("p n t -> p (n t)"),
             )
 
         layer1_product(0)
@@ -143,64 +160,64 @@ def tile_moe_ser_none_kernel(tc, x_words, x_scales, w1_words, w1_scales, w2, gat
             layer1_product(e)
             layer1_turn(e - 1)
         layer1_turn(E - 1)
-        g2 = gate_columns(g2rows, "g2")
-        for t in range(4):
-            layer1_scatter(t, 0, 0)
-        for e in range(1, E):
-            for t in range(2):
-                layer1_scatter(t, e, e)
+        for e in range(E):
+            layer1_planes(e, 1)
         w2_round(0)
-        pair_up(0)
-        pair_up(1)
-        for t in range(2, 4):
-            layer1_scatter(t, 1, E - 1)
-            pair_up(t)
+        w2rest = keep.tile([P, E - 1, N, 4], BF16, name="w2rest", tag="hrow3", align_bytes=64)
+        w2b.extend(w2rest[:, f] for f in range(E - 1))
+        for first, last in ((0, 0), (1, 1), (2, 3)):
+            for t in range(2):
+                layer1_scatter(t, first, last)
+        w2_round(1)
+        w2_round(2)
+        for t in range(3):
+            if t == 2:
+                layer1_scatter(t, 0, E - 1)
+            nc.scalar.copy(cround[t][:], ctok[t][:, 0:T])
+            layer2_gather(t, 0, 1)
+            layer2_gather(t, 2, 3)
+            if t == 1:
+                w2_round(3)
+        layer1_scatter(3, 0, E - 1)
+        nc.vector.tensor_copy(cround[3][:], ctok[3][:, 0:T])
 
-        cg = keep.tile([P, T, 2], U32, name="cg", align_bytes=64)
         cw = keep.tile([P, T], U32, name="cw", align_bytes=64)
         cs = keep.tile([P, T], U8, name="cs", align_bytes=64)
-        yrow = [keep.tile([P, N], F32, name="yrow%d" % f, align_bytes=64) for f in range(E)]
         ycol = keep.tile([P, 2, T], F32, name="ycol", align_bytes=64)
         otok = [keep.tile([P, T], F32, name="otok%d" % v, align_bytes=64) for v in range(2)]
-
-        def layer2_gather(f, u):
-            nc.vector.tensor_copy(cg[:, slots(f), u], cpair[u][:].rearrange("p s d -> p (s d)").bitcast(U32).indirect(list2[:, entries(f)]))
 
         def layer2_product(f):
             nc.vector.quantize_mx(
                 out=cw[:, slots(f)].bitcast(FP8X4),
                 scales=cs[:, slots(f)],
-                in_=cg[:, slots(f), :].rearrange("p s u -> p (s u)").bitcast(BF16),
+                in_=cg[:, slots(f), :].rearrange("p s t -> p (s t)"),
             )
-            bank = psum.tile([P, 512], F32, name="bank", tag="bank")
-            nc.tensor.matmul_mx(
-                out=bank[:, 0:N],
-                lhsT=cw[:, slots(f)].bitcast(FP8X4),
-                lhsT_scale=cs[:, slots(f)],
-                rhs=w2w[:, f, :].bitcast(FP8X4),
-                rhs_scale=w2s[:, f, :],
-                start=True,
-                stop=True,
-            )
-            nc.scalar.activation(out=yrow[f][:], in_=bank[:, 0:N], func=COPY, scale=g2[:, f : f + 1])
-
-        def layer2_turn(f):
             bank = psum.tile([P, 512], F32, name="bank", tag="bank")
             for v in range(2):
-                nc.tensor.transpose(bank[:, v * C : (v + 1) * C], yrow[f][:, v * P : (v + 1) * P], ident[:])
+                nc.tensor.matmul_mx(
+                    out=bank[:, v * C : (v + 1) * C],
+                    lhsT=w2w[:, f, v * P : (v + 1) * P].bitcast(FP8X4),
+                    lhsT_scale=w2s[:, f, v * P : (v + 1) * P],
+                    rhs=cw[:, slots(f)].bitcast(FP8X4),
+                    rhs_scale=cs[:, slots(f)],
+                    start=True,
+                    stop=True,
+                )
             nc.scalar.copy(ycol[:, :, slots(f)], bank[:, 0 : 2 * C].rearrange("p (v s) -> p v s", v=2))
 
-        for f in range(1, E):
-            w2_round(f)
         for f in range(E):
-            layer2_gather(f, 0)
+            layer2_gather(3, f, f)
         for f in range(E):
-            layer2_gather(f, 1)
             w2_quantise(f)
             layer2_product(f)
-            layer2_turn(f)
-        for f in range(E):
+        for first, last in ((0, 0), (1, 1), (2, 3)):
             for v in range(2):
-                nc.vector.tensor_copy(otok[v][:].indirect(list2[:, entries(f)]), ycol[:, v, slots(f)])
+                cols = slice(first * C, (last + 1) * C)
+                nc.vector.tensor_tensor(
+                    otok[v][:].indirect(list2[:, first * LIST_COLS : (last + 1) * LIST_COLS]),
+                    ycol[:, v, cols],
+                    g2[:, cols],
+                    mybir.AluOpType.mult,
+                )
         for v in range(2):
             nc.sync.dma_start(out[v * P : (v + 1) * P, :], otok[v][:])

@@ -29,7 +29,7 @@ def tile_moe_ser_none_kernel(tc, x_words, x_scales, w1_words, w1_scales, w2, gat
     nc = tc.nc
     with ExitStack() as ctx:
         keep = ctx.enter_context(tc.tile_pool(name="keep", bufs=1))
-        psum = ctx.enter_context(tc.psum_pool(name="psum", bufs=8))
+        psum = ctx.enter_context(tc.psum_pool(name="psum", bufs=1))
 
         def slots(e):
             return slice(e * C, (e + 1) * C)
@@ -55,7 +55,7 @@ def tile_moe_ser_none_kernel(tc, x_words, x_scales, w1_words, w1_scales, w2, gat
         nc.sync.dma_start(list1[:], offs)
         nc.sync.dma_start(xw[:], x_words[0].rearrange("p t d -> p (t d)").bitcast(I32))
         for r in range(4):
-            nc.scalar.dma_start(xs[r:P:32, :].bitcast(I32), xs_rows[r].bitcast(I32))
+            nc.sync.dma_start(xs[r:P:32, :].bitcast(I32), xs_rows[r].bitcast(I32))
         nc.sync.dma_start(g1rows[:], gate1[0:32, :].rearrange("r (e c) -> (r e) c", c=C))
         nc.sync.dma_start(w1first[:].bitcast(I32), w1_words[0, 0].bitcast(I32))
         for r in range(4):
@@ -67,7 +67,7 @@ def tile_moe_ser_none_kernel(tc, x_words, x_scales, w1_words, w1_scales, w2, gat
         nc.sync.dma_start(list2[:], offs2)
 
         def gate_columns(rows, name):
-            bank = psum.tile([P, 512], F32, name="bank", tag="bank")
+            bank = psum.tile([P, 512], F32, name="gate_bank", tag="a")
             nc.tensor.transpose(bank[:, 0:P], rows[:], ident[:])
             cols = keep.tile([P, E], F32, name=name)
             nc.scalar.copy(cols[:], bank[:, 0:E])
@@ -85,50 +85,41 @@ def tile_moe_ser_none_kernel(tc, x_words, x_scales, w1_words, w1_scales, w2, gat
         xgw = keep.tile([P, T], U32, name="xgw", align_bytes=64)
         xgs = keep.tile([P, T], U8, name="xgs", align_bytes=64)
         hrow = [keep.tile([P, 2, P, 2], BF16, name="hrow%d" % e, tag="hrow%d" % e, align_bytes=64) for e in range(E)]
-        hcol = keep.tile([P, 4, T], F32, name="hcol", align_bytes=64)
+        hearly = [keep.tile([P, 2, C], F32, name="hearly%d" % e, align_bytes=64) for e in range(E)]
+        hlate = [keep.tile([P, T], F32, name="hlate%d" % d, align_bytes=64) for d in range(2)]
         ctok = [keep.tile([P, T if t < 2 else WIDE], F32, name="ctok%d" % t, align_bytes=64) for t in range(4)]
-        cround = [keep.tile([P, T], BF16, name="cround%d" % t, align_bytes=64) for t in range(4)]
+        cround = [keep.tile([P, WIDE if t < 3 else T], BF16, name="cround%d" % t, align_bytes=64) for t in range(4)]
         cg = keep.tile([P, T, 4], BF16, name="cg", align_bytes=64)
 
-        def layer1_product(e):
+        def layer1_gather(e):
             nc.vector.tensor_copy(xgw[:, slots(e)], xw[:].bitcast(U32).indirect(list1[:, entries(e)]))
             nc.vector.tensor_copy(xgs[:, slots(e)], xs[:].indirect(list1[:, entries(e)]))
-            bank = psum.tile([P, 512], F32, name="bank", tag="bank")
+
+        def layer1_product(e, first, width, tag):
+            bank = psum.tile([P, width], F32, name="h_bank", tag=tag)
             nc.tensor.matmul_mx(
                 out=bank[:],
                 lhsT=xgw[:, slots(e)].bitcast(FP8X4),
                 lhsT_scale=xgs[:, slots(e)],
-                rhs=w1w[e].bitcast(FP4X4),
-                rhs_scale=w1s[:, e, :],
+                rhs=w1w[e][:, 2 * first : 2 * (first + width)].bitcast(FP4X4),
+                rhs_scale=w1s[:, e, first : first + width],
                 start=True,
                 stop=True,
             )
-            nc.scalar.activation(
-                out=hrow[e][:],
-                in_=bank[:].rearrange("s (p u d) -> s u p d", u=2, d=2),
-                func=COPY,
-                scale=g1[:, e : e + 1],
-            )
+            return hrow[e][:, :, first // 4 : (first + width) // 4, :], bank[:].rearrange("s (p u d) -> s u p d", u=2, d=2)
 
-        turned = []
+        def gate_on_scalar(e, rows, sums):
+            nc.scalar.activation(out=rows, in_=sums, func=COPY, scale=g1[:, e : e + 1])
 
-        def layer1_turn(e):
-            bank = psum.tile([P, 512], F32, name="bank", tag="bank")
+        def gate_on_vector(e, rows, sums):
+            nc.vector.tensor_scalar(out=rows, in0=sums, scalar1=g1[:, e : e + 1], scalar2=None, op0=mybir.AluOpType.mult)
+
+        def layer1_turn(e, u, bank):
             words = hrow[e][:].rearrange("s u p d -> s (u p d)").bitcast(F32)
-            for u in range(2):
-                nc.tensor.transpose(bank[:, u * C : (u + 1) * C], words[:, u * P : (u + 1) * P], ident[:])
-            turned.append(bank)
-            layer1_planes(e, 0)
+            nc.tensor.transpose(bank, words[:, u * P : (u + 1) * P], ident[:])
 
-        def layer1_planes(e, u):
-            pairs = turned[e][:, u * C : (u + 1) * C].bitcast(BF16).rearrange("p (s d) -> p d s", d=2)
-            nc.scalar.copy(hcol[:, 2 * u : 2 * u + 2, slots(e)], pairs)
-
-        def layer1_scatter(t, first, last):
-            nc.vector.tensor_copy(
-                ctok[t][:].indirect(list1[:, first * LIST_COLS : (last + 1) * LIST_COLS]),
-                hcol[:, t, first * C : (last + 1) * C],
-            )
+        def planes(bank):
+            return bank.bitcast(BF16).rearrange("p (s d) -> p d s", d=2)
 
         def layer2_gather(t, first, last):
             nc.scalar.activation(
@@ -137,7 +128,7 @@ def tile_moe_ser_none_kernel(tc, x_words, x_scales, w1_words, w1_scales, w2, gat
                 func=COPY,
             )
 
-        w2b = [keep.tile([P, N, 4], BF16, name="w2b0", align_bytes=64)[:]]
+        w2b = [keep.tile([P, N, 4], BF16, name="w2first", align_bytes=64)[:]]
         w2w = keep.tile([P, E, N], U32, name="w2w", align_bytes=64)
         w2s = keep.tile([P, E, N], U8, name="w2s", align_bytes=64)
 
@@ -155,35 +146,48 @@ def tile_moe_ser_none_kernel(tc, x_words, x_scales, w1_words, w1_scales, w2, gat
                 in_=w2b[f].rearrange("p n t -> p (n t)"),
             )
 
-        layer1_product(0)
-        for e in range(1, E):
-            layer1_product(e)
-            layer1_turn(e - 1)
-        layer1_turn(E - 1)
+        layer1_gather(0)
+        low = layer1_product(0, 0, H // 2, "a")
+        high = layer1_product(0, H // 2, H // 2, "b")
+        layer1_gather(1)
+        gate_on_scalar(0, *low)
+        gate_on_vector(0, *high)
+        late_bank = psum.tile([P, T], F32, name="late_bank", tag="late")
         for e in range(E):
-            layer1_planes(e, 1)
+            if e > 0:
+                if e > 1:
+                    layer1_gather(e)
+                gate_on_scalar(e, *layer1_product(e, 0, H, ("b", "c", "b")[e - 1]))
+            early_bank = psum.tile([P, C], F32, name="early_bank", tag=("c", "d", "e", "f")[e])
+            layer1_turn(e, 0, early_bank[:])
+            nc.scalar.copy(hearly[e][:], planes(early_bank[:]))
+            layer1_turn(e, 1, late_bank[:, slots(e)])
+        for d in range(2):
+            nc.scalar.copy(hlate[d][:], planes(late_bank[:])[:, d, :])
+        w2held = keep.tile([P, E - 1, N, 4], BF16, name="w2held", tag="hrow3", align_bytes=64)
+        w2b.extend(w2held[:, f] for f in range(E - 1))
         w2_round(0)
-        w2rest = keep.tile([P, E - 1, N, 4], BF16, name="w2rest", tag="hrow3", align_bytes=64)
-        w2b.extend(w2rest[:, f] for f in range(E - 1))
-        for first, last in ((0, 0), (1, 1), (2, 3)):
-            for t in range(2):
-                layer1_scatter(t, first, last)
-        w2_round(1)
-        w2_round(2)
+        for e, t in ((0, 0), (0, 1), (1, 0), (2, 0), (3, 0), (1, 1), (2, 1), (3, 1)):
+            nc.vector.tensor_copy(ctok[t][:].indirect(list1[:, entries(e)]), hearly[e][:, t, :])
         for t in range(3):
             if t == 2:
-                layer1_scatter(t, 0, E - 1)
-            nc.scalar.copy(cround[t][:], ctok[t][:, 0:T])
-            layer2_gather(t, 0, 1)
-            layer2_gather(t, 2, 3)
-            if t == 1:
-                w2_round(3)
-        layer1_scatter(3, 0, E - 1)
+                nc.vector.tensor_copy(ctok[2][:].indirect(list1[:]), hlate[0][:])
+            w2_round(t + 1)
+            nc.gpsimd.tensor_scalar(
+                out=cround[t][:, 0:T],
+                in0=ctok[t][:, 0:T],
+                scalar1=1.0,
+                scalar2=0.0,
+                op0=mybir.AluOpType.mult,
+                op1=mybir.AluOpType.add,
+            )
+            layer2_gather(t, 0, E - 1)
+        nc.vector.tensor_copy(ctok[3][:].indirect(list1[:]), hlate[1][:])
         nc.vector.tensor_copy(cround[3][:], ctok[3][:, 0:T])
 
         cw = keep.tile([P, T], U32, name="cw", align_bytes=64)
         cs = keep.tile([P, T], U8, name="cs", align_bytes=64)
-        ycol = keep.tile([P, 2, T], F32, name="ycol", align_bytes=64)
+        ycol = [keep.tile([P, 2, C], F32, name="ycol%d" % f, align_bytes=64) for f in range(E)]
         otok = [keep.tile([P, T], F32, name="otok%d" % v, align_bytes=64) for v in range(2)]
 
         def layer2_product(f):
@@ -192,7 +196,7 @@ def tile_moe_ser_none_kernel(tc, x_words, x_scales, w1_words, w1_scales, w2, gat
                 scales=cs[:, slots(f)],
                 in_=cg[:, slots(f), :].rearrange("p s t -> p (s t)"),
             )
-            bank = psum.tile([P, 512], F32, name="bank", tag="bank")
+            bank = psum.tile([P, 2 * C], F32, name="y_bank", tag=("a", "b", "c", "g")[f])
             for v in range(2):
                 nc.tensor.matmul_mx(
                     out=bank[:, v * C : (v + 1) * C],
@@ -203,21 +207,25 @@ def tile_moe_ser_none_kernel(tc, x_words, x_scales, w1_words, w1_scales, w2, gat
                     start=True,
                     stop=True,
                 )
-            nc.scalar.copy(ycol[:, :, slots(f)], bank[:, 0 : 2 * C].rearrange("p (v s) -> p v s", v=2))
+            return bank
 
-        for f in range(E):
-            layer2_gather(3, f, f)
+        layer2_gather(3, 0, 0)
         for f in range(E):
             w2_quantise(f)
-            layer2_product(f)
-        for first, last in ((0, 0), (1, 1), (2, 3)):
-            for v in range(2):
-                cols = slice(first * C, (last + 1) * C)
-                nc.vector.tensor_tensor(
-                    otok[v][:].indirect(list2[:, first * LIST_COLS : (last + 1) * LIST_COLS]),
-                    ycol[:, v, cols],
-                    g2[:, cols],
-                    mybir.AluOpType.mult,
-                )
+            bank = layer2_product(f)
+            if f + 1 < E:
+                layer2_gather(3, f + 1, f + 1)
+            if f == 0:
+                for v in range(2):
+                    nc.vector.tensor_copy(ycol[f][:, v, :], bank[:, v * C : (v + 1) * C])
+            else:
+                nc.scalar.copy(ycol[f][:].rearrange("p v s -> p (v s)"), bank[:])
+        for f, v in ((0, 0), (0, 1), (1, 0), (1, 1), (2, 0), (3, 0), (2, 1), (3, 1)):
+            nc.vector.tensor_tensor(
+                otok[v][:].indirect(list2[:, entries(f)]),
+                ycol[f][:, v, :],
+                g2[:, slots(f)],
+                mybir.AluOpType.mult,
+            )
         for v in range(2):
             nc.sync.dma_start(out[v * P : (v + 1) * P, :], otok[v][:])

@@ -21,6 +21,7 @@ E = 4
 C = 128
 LIST_COLS = C // 16
 WIDE = 704
+GROUPS = ((0, 0), (1, 1), (2, 3))
 
 FLOPS = 2 * T * 512 * H + 2 * T * H * N
 
@@ -85,7 +86,7 @@ def tile_moe_ser_none_kernel(tc, x_words, x_scales, w1_words, w1_scales, w2, gat
         xgw = keep.tile([P, T], U32, name="xgw", align_bytes=64)
         xgs = keep.tile([P, T], U8, name="xgs", align_bytes=64)
         hrow = [keep.tile([P, 2, P, 2], BF16, name="hrow%d" % e, tag="hrow%d" % e, align_bytes=64) for e in range(E)]
-        hearly = [keep.tile([P, 2, C], F32, name="hearly%d" % e, align_bytes=64) for e in range(E)]
+        hearly = keep.tile([P, 2, T], F32, name="hearly", align_bytes=64)
         hlate = [keep.tile([P, T], F32, name="hlate%d" % d, align_bytes=64) for d in range(2)]
         ctok = [keep.tile([P, T if t < 2 else WIDE], F32, name="ctok%d" % t, align_bytes=64) for t in range(4)]
         cround = [keep.tile([P, WIDE if t < 3 else T], BF16, name="cround%d" % t, align_bytes=64) for t in range(4)]
@@ -133,7 +134,7 @@ def tile_moe_ser_none_kernel(tc, x_words, x_scales, w1_words, w1_scales, w2, gat
         w2s = keep.tile([P, E, N], U8, name="w2s", align_bytes=64)
 
         def w2_round(f):
-            copy = nc.vector.tensor_copy if f == 0 else nc.scalar.copy
+            copy = nc.vector.tensor_copy if f in (0, 3) else nc.scalar.copy
             copy(
                 w2b[f].rearrange("p (c i) t -> p c t i", i=4),
                 w2raw[f].rearrange("p t (c i) -> p c t i", i=4),
@@ -160,34 +161,32 @@ def tile_moe_ser_none_kernel(tc, x_words, x_scales, w1_words, w1_scales, w2, gat
                 gate_on_scalar(e, *layer1_product(e, 0, H, ("b", "c", "b")[e - 1]))
             early_bank = psum.tile([P, C], F32, name="early_bank", tag=("c", "d", "e", "f")[e])
             layer1_turn(e, 0, early_bank[:])
-            nc.scalar.copy(hearly[e][:], planes(early_bank[:]))
+            nc.scalar.copy(hearly[:, :, slots(e)], planes(early_bank[:]))
             layer1_turn(e, 1, late_bank[:, slots(e)])
         for d in range(2):
             nc.scalar.copy(hlate[d][:], planes(late_bank[:])[:, d, :])
         w2held = keep.tile([P, E - 1, N, 4], BF16, name="w2held", tag="hrow3", align_bytes=64)
         w2b.extend(w2held[:, f] for f in range(E - 1))
         w2_round(0)
-        for e, t in ((0, 0), (0, 1), (1, 0), (2, 0), (3, 0), (1, 1), (2, 1), (3, 1)):
-            nc.vector.tensor_copy(ctok[t][:].indirect(list1[:, entries(e)]), hearly[e][:, t, :])
+        for first, last in GROUPS:
+            for t in range(2):
+                nc.vector.tensor_copy(
+                    ctok[t][:].indirect(list1[:, first * LIST_COLS : (last + 1) * LIST_COLS]),
+                    hearly[:, t, first * C : (last + 1) * C],
+                )
+        for f in range(1, E):
+            w2_round(f)
         for t in range(3):
             if t == 2:
                 nc.vector.tensor_copy(ctok[2][:].indirect(list1[:]), hlate[0][:])
-            w2_round(t + 1)
-            nc.gpsimd.tensor_scalar(
-                out=cround[t][:, 0:T],
-                in0=ctok[t][:, 0:T],
-                scalar1=1.0,
-                scalar2=0.0,
-                op0=mybir.AluOpType.mult,
-                op1=mybir.AluOpType.add,
-            )
+            nc.scalar.copy(cround[t][:, 0:T], ctok[t][:, 0:T])
             layer2_gather(t, 0, E - 1)
         nc.vector.tensor_copy(ctok[3][:].indirect(list1[:]), hlate[1][:])
         nc.vector.tensor_copy(cround[3][:], ctok[3][:, 0:T])
 
         cw = keep.tile([P, T], U32, name="cw", align_bytes=64)
         cs = keep.tile([P, T], U8, name="cs", align_bytes=64)
-        ycol = [keep.tile([P, 2, C], F32, name="ycol%d" % f, align_bytes=64) for f in range(E)]
+        ycol = keep.tile([P, 2, T], F32, name="ycol", align_bytes=64)
         otok = [keep.tile([P, T], F32, name="otok%d" % v, align_bytes=64) for v in range(2)]
 
         def layer2_product(f):
@@ -217,15 +216,17 @@ def tile_moe_ser_none_kernel(tc, x_words, x_scales, w1_words, w1_scales, w2, gat
                 layer2_gather(3, f + 1, f + 1)
             if f == 0:
                 for v in range(2):
-                    nc.vector.tensor_copy(ycol[f][:, v, :], bank[:, v * C : (v + 1) * C])
+                    nc.vector.tensor_copy(ycol[:, v, slots(f)], bank[:, v * C : (v + 1) * C])
             else:
-                nc.scalar.copy(ycol[f][:].rearrange("p v s -> p (v s)"), bank[:])
-        for f, v in ((0, 0), (0, 1), (1, 0), (1, 1), (2, 0), (3, 0), (2, 1), (3, 1)):
-            nc.vector.tensor_tensor(
-                otok[v][:].indirect(list2[:, entries(f)]),
-                ycol[f][:, v, :],
-                g2[:, slots(f)],
-                mybir.AluOpType.mult,
-            )
+                nc.scalar.copy(ycol[:, :, slots(f)], bank[:].rearrange("p (v s) -> p v s", v=2))
+        for first, last in GROUPS:
+            cols = slice(first * C, (last + 1) * C)
+            for v in range(2):
+                nc.vector.tensor_tensor(
+                    otok[v][:].indirect(list2[:, first * LIST_COLS : (last + 1) * LIST_COLS]),
+                    ycol[:, v, cols],
+                    g2[:, cols],
+                    mybir.AluOpType.mult,
+                )
         for v in range(2):
             nc.sync.dma_start(out[v * P : (v + 1) * P, :], otok[v][:])

@@ -133,12 +133,25 @@ def tile_moe_ser_none_kernel(tc, x_words, x_scales, w1_words, w1_scales, w2, gat
         w2w = keep.tile([P, E, N], U32, name="w2w", align_bytes=64)
         w2s = keep.tile([P, E, N], U8, name="w2s", align_bytes=64)
 
-        def w2_round(f):
-            copy = nc.vector.tensor_copy if f in (0, 3) else nc.scalar.copy
-            copy(
-                w2b[f].rearrange("p (c i) t -> p c t i", i=4),
-                w2raw[f].rearrange("p t (c i) -> p c t i", i=4),
+        def gpsimd_round(rounded, values):
+            nc.gpsimd.tensor_scalar(
+                out=rounded,
+                in0=values,
+                scalar1=1.0,
+                scalar2=0.0,
+                op0=mybir.AluOpType.mult,
+                op1=mybir.AluOpType.add,
             )
+
+        def w2_round(f):
+            if f == E - 1:
+                gpsimd_round(w2b[f], w2raw[f].rearrange("p t n -> p n t"))
+            else:
+                copy = nc.vector.tensor_copy if f == 0 else nc.scalar.copy
+                copy(
+                    w2b[f].rearrange("p (c i) t -> p c t i", i=4),
+                    w2raw[f].rearrange("p t (c i) -> p c t i", i=4),
+                )
 
         def w2_quantise(f):
             nc.vector.quantize_mx(
@@ -179,7 +192,7 @@ def tile_moe_ser_none_kernel(tc, x_words, x_scales, w1_words, w1_scales, w2, gat
         for t in range(3):
             if t == 2:
                 nc.vector.tensor_copy(ctok[2][:].indirect(list1[:]), hlate[0][:])
-            nc.scalar.copy(cround[t][:, 0:T], ctok[t][:, 0:T])
+            gpsimd_round(cround[t][:, 0:T], ctok[t][:, 0:T])
             layer2_gather(t, 0, E - 1)
         nc.vector.tensor_copy(ctok[3][:].indirect(list1[:]), hlate[1][:])
         nc.vector.tensor_copy(cround[3][:], ctok[3][:, 0:T])

@@ -20,7 +20,6 @@ N = 256
 E = 4
 C = 128
 LIST_COLS = C // 16
-WIDE = 704
 GROUPS = ((0, 0), (1, 1), (2, 3))
 
 FLOPS = 2 * T * 512 * H + 2 * T * H * N
@@ -86,11 +85,12 @@ def tile_moe_ser_none_kernel(tc, x_words, x_scales, w1_words, w1_scales, w2, gat
         xgw = keep.tile([P, T], U32, name="xgw", align_bytes=64)
         xgs = keep.tile([P, T], U8, name="xgs", align_bytes=64)
         hrow = [keep.tile([P, 2, P, 2], BF16, name="hrow%d" % e, tag="hrow%d" % e, align_bytes=64) for e in range(E)]
-        hearly = keep.tile([P, 2, T], F32, name="hearly", align_bytes=64)
-        hlate = [keep.tile([P, T], F32, name="hlate%d" % d, align_bytes=64) for d in range(2)]
-        ctok = [keep.tile([P, T if t < 2 else WIDE], F32, name="ctok%d" % t, align_bytes=64) for t in range(4)]
-        cround = [keep.tile([P, WIDE if t < 3 else T], BF16, name="cround%d" % t, align_bytes=64) for t in range(4)]
-        cg = keep.tile([P, T, 4], BF16, name="cg", align_bytes=64)
+        hfirst = keep.tile([P, 2, C], F32, name="hfirst", align_bytes=64)
+        hearly = keep.tile([P, T - C], F32, name="hearly", align_bytes=64)
+        hlate = keep.tile([P, T - C], F32, name="hlate", align_bytes=64)
+        ctok = [keep.tile([P, T], F32, name="ctok%d" % u, align_bytes=64) for u in range(2)]
+        cplane = [keep.tile([P, T], BF16, name="cplane%d" % d, align_bytes=64) for d in range(2)]
+        cg = [keep.tile([P, C, 4], BF16, name="cg%d" % f, align_bytes=64) for f in range(E)]
 
         def layer1_gather(e):
             nc.vector.tensor_copy(xgw[:, slots(e)], xw[:].bitcast(U32).indirect(list1[:, entries(e)]))
@@ -119,15 +119,11 @@ def tile_moe_ser_none_kernel(tc, x_words, x_scales, w1_words, w1_scales, w2, gat
             words = hrow[e][:].rearrange("s u p d -> s (u p d)").bitcast(F32)
             nc.tensor.transpose(bank, words[:, u * P : (u + 1) * P], ident[:])
 
-        def planes(bank):
-            return bank.bitcast(BF16).rearrange("p (s d) -> p d s", d=2)
-
-        def layer2_gather(t, first, last):
-            nc.scalar.activation(
-                out=cg[:, first * C : (last + 1) * C, t],
-                in_=cround[t][:].indirect(list2[:, first * LIST_COLS : (last + 1) * LIST_COLS]),
-                func=COPY,
-            )
+        def layer2_gather(f):
+            for d in range(2):
+                nc.scalar.activation(out=cg[f][:, :, d], in_=cplane[d][:].indirect(list2[:, entries(f)]), func=COPY)
+            words = cg[f][:].rearrange("p s t -> p (s t)").bitcast(U32).rearrange("p (s u) -> p s u", u=2)
+            nc.vector.tensor_copy(words[:, :, 1], ctok[1][:].bitcast(U32).indirect(list2[:, entries(f)]))
 
         w2b = [keep.tile([P, N, 4], BF16, name="w2first", align_bytes=64)[:]]
         w2w = keep.tile([P, E, N], U32, name="w2w", align_bytes=64)
@@ -144,7 +140,7 @@ def tile_moe_ser_none_kernel(tc, x_words, x_scales, w1_words, w1_scales, w2, gat
             )
 
         def w2_round(f):
-            if f == E - 1:
+            if f >= 2:
                 gpsimd_round(w2b[f], w2raw[f].rearrange("p t n -> p n t"))
             else:
                 copy = nc.vector.tensor_copy if f == 0 else nc.scalar.copy
@@ -166,36 +162,33 @@ def tile_moe_ser_none_kernel(tc, x_words, x_scales, w1_words, w1_scales, w2, gat
         layer1_gather(1)
         gate_on_scalar(0, *low)
         gate_on_vector(0, *high)
-        late_bank = psum.tile([P, T], F32, name="late_bank", tag="late")
-        for e in range(E):
-            if e > 0:
-                if e > 1:
-                    layer1_gather(e)
-                gate_on_scalar(e, *layer1_product(e, 0, H, ("b", "c", "b")[e - 1]))
-            early_bank = psum.tile([P, C], F32, name="early_bank", tag=("c", "d", "e", "f")[e])
+        first_bank = psum.tile([P, 2 * C], F32, name="first_bank", tag="c")
+        for u in range(2):
+            layer1_turn(0, u, first_bank[:, slots(u)])
+        nc.scalar.copy(hfirst[:].rearrange("p u s -> p (u s)"), first_bank[:])
+        late_bank = psum.tile([P, T - C], F32, name="late_bank", tag="late")
+        for e in range(1, E):
+            if e > 1:
+                layer1_gather(e)
+            gate_on_scalar(e, *layer1_product(e, 0, H, ("b", "c", "b")[e - 1]))
+            early_bank = psum.tile([P, C], F32, name="early_bank", tag=("d", "e", "f")[e - 1])
             layer1_turn(e, 0, early_bank[:])
-            nc.scalar.copy(hearly[:, :, slots(e)], planes(early_bank[:]))
-            layer1_turn(e, 1, late_bank[:, slots(e)])
-        for d in range(2):
-            nc.scalar.copy(hlate[d][:], planes(late_bank[:])[:, d, :])
+            nc.scalar.copy(hearly[:, slots(e - 1)], early_bank[:])
+            layer1_turn(e, 1, late_bank[:, slots(e - 1)])
+        nc.scalar.copy(hlate[:], late_bank[:])
         w2held = keep.tile([P, E - 1, N, 4], BF16, name="w2held", tag="hrow3", align_bytes=64)
         w2b.extend(w2held[:, f] for f in range(E - 1))
         w2_round(0)
-        for first, last in GROUPS:
-            for t in range(2):
-                nc.vector.tensor_copy(
-                    ctok[t][:].indirect(list1[:, first * LIST_COLS : (last + 1) * LIST_COLS]),
-                    hearly[:, t, first * C : (last + 1) * C],
-                )
+        for u in range(2):
+            nc.vector.tensor_copy(ctok[u][:].indirect(list1[:, entries(0)]), hfirst[:, u, :])
+        nc.vector.tensor_copy(ctok[0][:].indirect(list1[:, entries(1)]), hearly[:, 0:C])
+        nc.vector.tensor_copy(ctok[0][:].indirect(list1[:, 2 * LIST_COLS :]), hearly[:, C:])
         for f in range(1, E):
             w2_round(f)
-        for t in range(3):
-            if t == 2:
-                nc.vector.tensor_copy(ctok[2][:].indirect(list1[:]), hlate[0][:])
-            gpsimd_round(cround[t][:, 0:T], ctok[t][:, 0:T])
-            layer2_gather(t, 0, E - 1)
-        nc.vector.tensor_copy(ctok[3][:].indirect(list1[:]), hlate[1][:])
-        nc.vector.tensor_copy(cround[3][:], ctok[3][:, 0:T])
+        nc.vector.tensor_copy(ctok[1][:].indirect(list1[:, LIST_COLS:]), hlate[:])
+        pairs = ctok[0][:].bitcast(BF16).rearrange("p (s d) -> p s d", d=2)
+        nc.scalar.copy(cplane[0][:], pairs[:, :, 0])
+        gpsimd_round(cplane[1][:], pairs[:, :, 1])
 
         cw = keep.tile([P, T], U32, name="cw", align_bytes=64)
         cs = keep.tile([P, T], U8, name="cs", align_bytes=64)
@@ -206,7 +199,7 @@ def tile_moe_ser_none_kernel(tc, x_words, x_scales, w1_words, w1_scales, w2, gat
             nc.vector.quantize_mx(
                 out=cw[:, slots(f)].bitcast(FP8X4),
                 scales=cs[:, slots(f)],
-                in_=cg[:, slots(f), :].rearrange("p s t -> p (s t)"),
+                in_=cg[f][:].rearrange("p s t -> p (s t)"),
             )
             bank = psum.tile([P, 2 * C], F32, name="y_bank", tag=("a", "b", "c", "g")[f])
             for v in range(2):
@@ -221,12 +214,12 @@ def tile_moe_ser_none_kernel(tc, x_words, x_scales, w1_words, w1_scales, w2, gat
                 )
             return bank
 
-        layer2_gather(3, 0, 0)
+        layer2_gather(0)
         for f in range(E):
             w2_quantise(f)
             bank = layer2_product(f)
             if f + 1 < E:
-                layer2_gather(3, f + 1, f + 1)
+                layer2_gather(f + 1)
             if f == 0:
                 for v in range(2):
                     nc.vector.tensor_copy(ycol[:, v, slots(f)], bank[:, v * C : (v + 1) * C])

@@ -20,7 +20,8 @@ N = 256
 E = 4
 C = 128
 LIST_COLS = C // 16
-GROUPS = ((0, 0), (1, 1), (2, 3))
+WIDE = 768
+PIECES = ((0, 0, 0), (1, 0, 0), (0, 1, 1), (0, 2, 3), (1, 1, 3))
 
 FLOPS = 2 * T * 512 * H + 2 * T * H * N
 
@@ -53,9 +54,9 @@ def tile_moe_ser_none_kernel(tc, x_words, x_scales, w1_words, w1_scales, w2, gat
         w1s_rows = w1_scales[:, 0].rearrange("e (q r) n -> r q e n", r=4)
         make_identity(nc, ident[:])
         nc.sync.dma_start(list1[:], offs)
-        nc.sync.dma_start(xw[:], x_words[0].rearrange("p t d -> p (t d)").bitcast(I32))
         for r in range(4):
             nc.sync.dma_start(xs[r:P:32, :].bitcast(I32), xs_rows[r].bitcast(I32))
+        nc.sync.dma_start(xw[:], x_words[0].rearrange("p t d -> p (t d)").bitcast(I32))
         nc.sync.dma_start(g1rows[:], gate1[0:32, :].rearrange("r (e c) -> (r e) c", c=C))
         nc.sync.dma_start(w1first[:].bitcast(I32), w1_words[0, 0].bitcast(I32))
         for r in range(4):
@@ -82,25 +83,25 @@ def tile_moe_ser_none_kernel(tc, x_words, x_scales, w1_words, w1_scales, w2, gat
             nc.sync.dma_start(w2raw[f], w2[f].rearrange("(p j) n -> p j n", j=4))
         nc.sync.dma_start(g2, gate2)
 
-        xgw = keep.tile([P, T], U32, name="xgw", align_bytes=64)
+        xgw = []
         xgs = keep.tile([P, T], U8, name="xgs", align_bytes=64)
         hrow = [keep.tile([P, 2, P, 2], BF16, name="hrow%d" % e, tag="hrow%d" % e, align_bytes=64) for e in range(E)]
-        hfirst = keep.tile([P, 2, C], F32, name="hfirst", align_bytes=64)
-        hearly = keep.tile([P, T - C], F32, name="hearly", align_bytes=64)
-        hlate = keep.tile([P, T - C], F32, name="hlate", align_bytes=64)
+        hboth = [keep.tile([P, 2 * C], F32, name="hboth%d" % e, align_bytes=64) for e in range(2)]
+        hlast = [keep.tile([P, 2 * C], F32, name="hlast%d" % u, tag="hlast%d" % u, align_bytes=64) for u in range(2)]
         ctok = [keep.tile([P, T], F32, name="ctok%d" % u, align_bytes=64) for u in range(2)]
         cplane = [keep.tile([P, T], BF16, name="cplane%d" % d, align_bytes=64) for d in range(2)]
-        cg = [keep.tile([P, C, 4], BF16, name="cg%d" % f, align_bytes=64) for f in range(E)]
+        cg = []
 
         def layer1_gather(e):
-            nc.vector.tensor_copy(xgw[:, slots(e)], xw[:].bitcast(U32).indirect(list1[:, entries(e)]))
+            xgw.append(keep.tile([P, C], U32, name="xgw%d" % e, tag="xgw%d" % (e % 3), align_bytes=64))
+            nc.vector.tensor_copy(xgw[e][:], xw[:].bitcast(U32).indirect(list1[:, entries(e)]))
             nc.vector.tensor_copy(xgs[:, slots(e)], xs[:].indirect(list1[:, entries(e)]))
 
         def layer1_product(e, first, width, tag):
             bank = psum.tile([P, width], F32, name="h_bank", tag=tag)
             nc.tensor.matmul_mx(
                 out=bank[:],
-                lhsT=xgw[:, slots(e)].bitcast(FP8X4),
+                lhsT=xgw[e][:].bitcast(FP8X4),
                 lhsT_scale=xgs[:, slots(e)],
                 rhs=w1w[e][:, 2 * first : 2 * (first + width)].bitcast(FP4X4),
                 rhs_scale=w1s[:, e, first : first + width],
@@ -120,13 +121,13 @@ def tile_moe_ser_none_kernel(tc, x_words, x_scales, w1_words, w1_scales, w2, gat
             nc.tensor.transpose(bank, words[:, u * P : (u + 1) * P], ident[:])
 
         def layer2_gather(f):
+            cg.append(keep.tile([P, C, 4], BF16, name="cg%d" % f, tag="cg%d" % f, align_bytes=64))
             for d in range(2):
                 nc.scalar.activation(out=cg[f][:, :, d], in_=cplane[d][:].indirect(list2[:, entries(f)]), func=COPY)
             words = cg[f][:].rearrange("p s t -> p (s t)").bitcast(U32).rearrange("p (s u) -> p s u", u=2)
-            nc.vector.tensor_copy(words[:, :, 1], ctok[1][:].bitcast(U32).indirect(list2[:, entries(f)]))
+            nc.vector.tensor_copy(words[:, :, 1], ctok[1][:, 0:T].bitcast(U32).indirect(list2[:, entries(f)]))
 
-        w2b = [keep.tile([P, N, 4], BF16, name="w2first", align_bytes=64)[:]]
-        w2w = keep.tile([P, E, N], U32, name="w2w", align_bytes=64)
+        w2w = []
         w2s = keep.tile([P, E, N], U8, name="w2s", align_bytes=64)
 
         def gpsimd_round(rounded, values):
@@ -139,100 +140,101 @@ def tile_moe_ser_none_kernel(tc, x_words, x_scales, w1_words, w1_scales, w2, gat
                 op1=mybir.AluOpType.add,
             )
 
-        def w2_round(f):
-            if f >= 2:
-                gpsimd_round(w2b[f], w2raw[f].rearrange("p t n -> p n t"))
-            else:
-                copy = nc.vector.tensor_copy if f == 0 else nc.scalar.copy
-                copy(
-                    w2b[f].rearrange("p (c i) t -> p c t i", i=4),
+        def w2_round(f, rounded):
+            if f == 1:
+                nc.scalar.copy(
+                    rounded.rearrange("p (c i) t -> p c t i", i=4),
                     w2raw[f].rearrange("p t (c i) -> p c t i", i=4),
                 )
+            else:
+                gpsimd_round(rounded, w2raw[f].rearrange("p t n -> p n t"))
 
-        def w2_quantise(f):
+        def w2_quantise(first, count, tag):
+            codes = keep.tile([P, count * N], U32, name="w2w%d" % first, tag=tag, align_bytes=64)
+            w2w.extend(codes[:, j * N : (j + 1) * N] for j in range(count))
             nc.vector.quantize_mx(
-                out=w2w[:, f, :].bitcast(FP8X4),
-                scales=w2s[:, f, :],
-                in_=w2b[f].rearrange("p n t -> p (n t)"),
+                out=codes[:].bitcast(FP8X4),
+                scales=w2s[:, first : first + count, :].rearrange("p f n -> p (f n)"),
+                in_=w2b[first][:].rearrange("p f n t -> p (f n t)"),
             )
 
         layer1_gather(0)
         low = layer1_product(0, 0, H // 2, "a")
         high = layer1_product(0, H // 2, H // 2, "b")
         layer1_gather(1)
-        gate_on_scalar(0, *low)
-        gate_on_vector(0, *high)
-        first_bank = psum.tile([P, 2 * C], F32, name="first_bank", tag="c")
+        gate_on_vector(0, *low)
+        gate_on_scalar(0, *high)
+        for e in range(2):
+            if e == 1:
+                gate_on_scalar(1, *layer1_product(1, 0, H, "c"))
+            both_bank = psum.tile([P, 2 * C], F32, name="both_bank", tag=("f", "g")[e])
+            for u in range(2):
+                layer1_turn(e, u, both_bank[:, slots(u)])
+            copy = nc.vector.tensor_copy if e == 0 else nc.scalar.copy
+            copy(hboth[e][:], both_bank[:])
+        last_banks = [psum.tile([P, 2 * C], F32, name="last_bank", tag=("d", "e")[u]) for u in range(2)]
+        for e in range(2, E):
+            layer1_gather(e)
+            gate_on_scalar(e, *layer1_product(e, 0, H, ("b", "a")[e - 2]))
+            for u in range(2):
+                layer1_turn(e, u, last_banks[u][:, slots(e - 2)])
         for u in range(2):
-            layer1_turn(0, u, first_bank[:, slots(u)])
-        nc.scalar.copy(hfirst[:].rearrange("p u s -> p (u s)"), first_bank[:])
-        late_bank = psum.tile([P, T - C], F32, name="late_bank", tag="late")
-        for e in range(1, E):
-            if e > 1:
-                layer1_gather(e)
-            gate_on_scalar(e, *layer1_product(e, 0, H, ("b", "c", "b")[e - 1]))
-            early_bank = psum.tile([P, C], F32, name="early_bank", tag=("d", "e", "f")[e - 1])
-            layer1_turn(e, 0, early_bank[:])
-            nc.scalar.copy(hearly[:, slots(e - 1)], early_bank[:])
-            layer1_turn(e, 1, late_bank[:, slots(e - 1)])
-        nc.scalar.copy(hlate[:], late_bank[:])
-        w2held = keep.tile([P, E - 1, N, 4], BF16, name="w2held", tag="hrow3", align_bytes=64)
-        w2b.extend(w2held[:, f] for f in range(E - 1))
-        w2_round(0)
+            nc.scalar.copy(hlast[u][:], last_banks[u][:])
+        for e in range(2):
+            for u in range(2):
+                nc.vector.tensor_copy(ctok[u][:].indirect(list1[:, entries(e)]), hboth[e][:, slots(u)])
         for u in range(2):
-            nc.vector.tensor_copy(ctok[u][:].indirect(list1[:, entries(0)]), hfirst[:, u, :])
-        nc.vector.tensor_copy(ctok[0][:].indirect(list1[:, entries(1)]), hearly[:, 0:C])
-        nc.vector.tensor_copy(ctok[0][:].indirect(list1[:, 2 * LIST_COLS :]), hearly[:, C:])
-        for f in range(1, E):
-            w2_round(f)
-        nc.vector.tensor_copy(ctok[1][:].indirect(list1[:, LIST_COLS:]), hlate[:])
+            nc.vector.tensor_copy(ctok[u][:].indirect(list1[:, 2 * LIST_COLS :]), hlast[u][:])
+        w2b = [
+            keep.tile([P, count, N, 4], BF16, name="w2b%d" % j, tag=tag, align_bytes=64)
+            for j, (count, tag) in enumerate(((1, "w2b0"), (1, "hrow3"), (2, "w2b2")))
+        ]
+        w2_round(0, w2b[0][:, 0])
+        w2_round(1, w2b[1][:, 0])
+        w2_round(2, w2b[2][:, 0])
+        w2_round(3, w2b[2][:, 1])
         pairs = ctok[0][:].bitcast(BF16).rearrange("p (s d) -> p s d", d=2)
-        nc.scalar.copy(cplane[0][:], pairs[:, :, 0])
-        gpsimd_round(cplane[1][:], pairs[:, :, 1])
+        for d in range(2):
+            nc.scalar.copy(cplane[d][:], pairs[:, :, d])
 
-        cw = keep.tile([P, T], U32, name="cw", align_bytes=64)
         cs = keep.tile([P, T], U8, name="cs", align_bytes=64)
         ycol = keep.tile([P, 2, T], F32, name="ycol", align_bytes=64)
-        otok = [keep.tile([P, T], F32, name="otok%d" % v, align_bytes=64) for v in range(2)]
+        otok = [keep.tile([P, (T, WIDE)[v]], F32, name="otok%d" % v, tag=("w2b2", "otok1")[v], align_bytes=64) for v in range(2)]
 
         def layer2_product(f):
+            cw = keep.tile([P, C], U32, name="cw%d" % f, tag="cw%d" % f, align_bytes=64)
             nc.vector.quantize_mx(
-                out=cw[:, slots(f)].bitcast(FP8X4),
+                out=cw[:].bitcast(FP8X4),
                 scales=cs[:, slots(f)],
                 in_=cg[f][:].rearrange("p s t -> p (s t)"),
             )
-            bank = psum.tile([P, 2 * C], F32, name="y_bank", tag=("a", "b", "c", "g")[f])
+            bank = psum.tile([P, 2 * C], F32, name="y_bank", tag=("a", "b", "c", "d")[f])
             for v in range(2):
                 nc.tensor.matmul_mx(
                     out=bank[:, v * C : (v + 1) * C],
-                    lhsT=w2w[:, f, v * P : (v + 1) * P].bitcast(FP8X4),
+                    lhsT=w2w[f][:, v * P : (v + 1) * P].bitcast(FP8X4),
                     lhsT_scale=w2s[:, f, v * P : (v + 1) * P],
-                    rhs=cw[:, slots(f)].bitcast(FP8X4),
+                    rhs=cw[:].bitcast(FP8X4),
                     rhs_scale=cs[:, slots(f)],
                     start=True,
                     stop=True,
                 )
             return bank
 
-        layer2_gather(0)
         for f in range(E):
-            w2_quantise(f)
+            layer2_gather(f)
+        for f in range(E):
+            if f < 3:
+                w2_quantise(f, (1, 1, 2)[f], ("hlast1", "cg0", "cg1")[f])
             bank = layer2_product(f)
-            if f + 1 < E:
-                layer2_gather(f + 1)
-            if f == 0:
-                for v in range(2):
-                    nc.vector.tensor_copy(ycol[:, v, slots(f)], bank[:, v * C : (v + 1) * C])
-            else:
-                nc.scalar.copy(ycol[:, :, slots(f)], bank[:].rearrange("p (v s) -> p v s", v=2))
-        for first, last in GROUPS:
+            nc.scalar.copy(ycol[:, :, slots(f)], bank[:].rearrange("p (v s) -> p v s", v=2))
+        for v, first, last in PIECES:
             cols = slice(first * C, (last + 1) * C)
-            for v in range(2):
-                nc.vector.tensor_tensor(
-                    otok[v][:].indirect(list2[:, first * LIST_COLS : (last + 1) * LIST_COLS]),
-                    ycol[:, v, cols],
-                    g2[:, cols],
-                    mybir.AluOpType.mult,
-                )
+            nc.vector.tensor_tensor(
+                otok[v][:].indirect(list2[:, first * LIST_COLS : (last + 1) * LIST_COLS]),
+                ycol[:, v, cols],
+                g2[:, cols],
+                mybir.AluOpType.mult,
+            )
         for v in range(2):
-            nc.sync.dma_start(out[v * P : (v + 1) * P, :], otok[v][:])
+            nc.sync.dma_start(out[v * P : (v + 1) * P, :], otok[v][:, 0:T])

@@ -141,7 +141,7 @@ def tile_moe_ser_none_kernel(tc, x_words, x_scales, w1_words, w1_scales, w2, gat
             )
 
         def w2_round(f, rounded):
-            if f == 1:
+            if f < 2:
                 nc.scalar.copy(
                     rounded.rearrange("p (c i) t -> p c t i", i=4),
                     w2raw[f].rearrange("p t (c i) -> p c t i", i=4),
@@ -155,7 +155,7 @@ def tile_moe_ser_none_kernel(tc, x_words, x_scales, w1_words, w1_scales, w2, gat
             nc.vector.quantize_mx(
                 out=codes[:].bitcast(FP8X4),
                 scales=w2s[:, first : first + count, :].rearrange("p f n -> p (f n)"),
-                in_=w2b[first][:].rearrange("p f n t -> p (f n t)"),
+                in_=w2b[first // 2][:, first % 2 : first % 2 + count].rearrange("p f n t -> p (f n t)"),
             )
 
         layer1_gather(0)
@@ -186,13 +186,11 @@ def tile_moe_ser_none_kernel(tc, x_words, x_scales, w1_words, w1_scales, w2, gat
         for u in range(2):
             nc.vector.tensor_copy(ctok[u][:].indirect(list1[:, 2 * LIST_COLS :]), hlast[u][:])
         w2b = [
-            keep.tile([P, count, N, 4], BF16, name="w2b%d" % j, tag=tag, align_bytes=64)
-            for j, (count, tag) in enumerate(((1, "w2b0"), (1, "hrow3"), (2, "w2b2")))
+            keep.tile([P, 2, N, 4], BF16, name="w2b%d" % j, tag=tag, align_bytes=64)
+            for j, tag in enumerate(("hrow3", "w2b2"))
         ]
-        w2_round(0, w2b[0][:, 0])
-        w2_round(1, w2b[1][:, 0])
-        w2_round(2, w2b[2][:, 0])
-        w2_round(3, w2b[2][:, 1])
+        for f in range(E):
+            w2_round(f, w2b[f // 2][:, f % 2])
         pairs = ctok[0][:].bitcast(BF16).rearrange("p (s d) -> p s d", d=2)
         for d in range(2):
             nc.scalar.copy(cplane[d][:], pairs[:, :, d])

@@ -20,8 +20,6 @@ N = 256
 E = 4
 C = 128
 LIST_COLS = C // 16
-WIDE = 768
-PIECES = ((0, 0, 0), (1, 0, 0), (0, 1, 1), (0, 2, 3), (1, 1, 3))
 
 FLOPS = 2 * T * 512 * H + 2 * T * H * N
 
@@ -44,7 +42,7 @@ def tile_moe_ser_none_kernel(tc, x_words, x_scales, w1_words, w1_scales, w2, gat
         xs = keep.tile([P, T], U8, name="xs", align_bytes=64)
         w1first = keep.tile([P, 2 * H], U8, name="w1first", align_bytes=64)
         w1s = keep.tile([P, E, H], U8, name="w1s", align_bytes=64)
-        g1rows = keep.tile([P, C], F32, name="g1rows", tag="late", align_bytes=64)
+        g1rows = keep.tile([P, C], F32, name="g1rows", align_bytes=64)
         ident = keep.tile([P, P], F32, name="ident")
 
         nc.gpsimd.memset(xs[:].bitcast(I32), 0)
@@ -76,9 +74,8 @@ def tile_moe_ser_none_kernel(tc, x_words, x_scales, w1_words, w1_scales, w2, gat
 
         g1 = gate_columns(g1rows, "g1")
 
-        late = keep.tile([P, E * 4 * N + T], F32, name="late", tag="late", align_bytes=64)
-        w2raw = [late[:, f * 4 * N : (f + 1) * 4 * N].rearrange("p (j n) -> p j n", j=4) for f in range(E)]
-        g2 = late[:, E * 4 * N : E * 4 * N + T]
+        w2raw = [keep.tile([P, 4, N], F32, name="w2raw%d" % f, tag="w2raw%d" % f, align_bytes=64)[:] for f in range(E)]
+        g2 = keep.tile([P, T], F32, name="g2", align_bytes=64)[:]
         for f in range(E):
             nc.sync.dma_start(w2raw[f], w2[f].rearrange("(p j) n -> p j n", j=4))
         nc.sync.dma_start(g2, gate2)
@@ -86,11 +83,13 @@ def tile_moe_ser_none_kernel(tc, x_words, x_scales, w1_words, w1_scales, w2, gat
         xgw = []
         xgs = keep.tile([P, T], U8, name="xgs", align_bytes=64)
         hrow = [keep.tile([P, 2, P, 2], BF16, name="hrow%d" % e, tag="hrow%d" % e, align_bytes=64) for e in range(E)]
-        hboth = [keep.tile([P, 2 * C], F32, name="hboth%d" % e, align_bytes=64) for e in range(2)]
-        hlast = [keep.tile([P, 2 * C], F32, name="hlast%d" % u, tag="hlast%d" % u, align_bytes=64) for u in range(2)]
+        hzero = keep.tile([P, C], F32, name="hzero", align_bytes=64)
+        hfront = keep.tile([P, C // 2], F32, name="hfront", align_bytes=64)
+        hone = keep.tile([P, C], F32, name="hone", align_bytes=64)
+        hlast = keep.tile([P, 2 * C], F32, name="hlast", align_bytes=64)
+        hlate = keep.tile([P, 3 * C], F32, name="hlate", tag="hlate", align_bytes=64)
         ctok = [keep.tile([P, T], F32, name="ctok%d" % u, align_bytes=64) for u in range(2)]
-        cplane = [keep.tile([P, T], BF16, name="cplane%d" % d, align_bytes=64) for d in range(2)]
-        cg = []
+        cg = [keep.tile([P, C, 4], BF16, name="cg%d" % f, tag="cg%d" % f, align_bytes=64) for f in range(E)]
 
         def layer1_gather(e):
             xgw.append(keep.tile([P, C], U32, name="xgw%d" % e, tag="xgw%d" % (e % 3), align_bytes=64))
@@ -120,10 +119,10 @@ def tile_moe_ser_none_kernel(tc, x_words, x_scales, w1_words, w1_scales, w2, gat
             words = hrow[e][:].rearrange("s u p d -> s (u p d)").bitcast(F32)
             nc.tensor.transpose(bank, words[:, u * P : (u + 1) * P], ident[:])
 
-        def layer2_gather(f):
-            cg.append(keep.tile([P, C, 4], BF16, name="cg%d" % f, tag="cg%d" % f, align_bytes=64))
-            for d in range(2):
-                nc.scalar.activation(out=cg[f][:, :, d], in_=cplane[d][:].indirect(list2[:, entries(f)]), func=COPY)
+        def layer2_gather_plane(f, d):
+            nc.scalar.activation(out=cg[f][:, :, d], in_=cplane[d][:].indirect(list2[:, entries(f)]), func=COPY)
+
+        def layer2_gather_words(f):
             words = cg[f][:].rearrange("p s t -> p (s t)").bitcast(U32).rearrange("p (s u) -> p s u", u=2)
             nc.vector.tensor_copy(words[:, :, 1], ctok[1][:, 0:T].bitcast(U32).indirect(list2[:, entries(f)]))
 
@@ -141,7 +140,7 @@ def tile_moe_ser_none_kernel(tc, x_words, x_scales, w1_words, w1_scales, w2, gat
             )
 
         def w2_round(f, rounded):
-            if f < 2:
+            if f == 0:
                 nc.scalar.copy(
                     rounded.rearrange("p (c i) t -> p c t i", i=4),
                     w2raw[f].rearrange("p t (c i) -> p c t i", i=4),
@@ -155,7 +154,7 @@ def tile_moe_ser_none_kernel(tc, x_words, x_scales, w1_words, w1_scales, w2, gat
             nc.vector.quantize_mx(
                 out=codes[:].bitcast(FP8X4),
                 scales=w2s[:, first : first + count, :].rearrange("p f n -> p (f n)"),
-                in_=w2b[first // 2][:, first % 2 : first % 2 + count].rearrange("p f n t -> p (f n t)"),
+                in_=w2b[first][:].rearrange("p f n t -> p (f n t)"),
             )
 
         layer1_gather(0)
@@ -164,40 +163,54 @@ def tile_moe_ser_none_kernel(tc, x_words, x_scales, w1_words, w1_scales, w2, gat
         layer1_gather(1)
         gate_on_vector(0, *low)
         gate_on_scalar(0, *high)
-        for e in range(2):
-            if e == 1:
-                gate_on_scalar(1, *layer1_product(1, 0, H, "c"))
-            both_bank = psum.tile([P, 2 * C], F32, name="both_bank", tag=("f", "g")[e])
-            for u in range(2):
-                layer1_turn(e, u, both_bank[:, slots(u)])
-            copy = nc.vector.tensor_copy if e == 0 else nc.scalar.copy
-            copy(hboth[e][:], both_bank[:])
-        last_banks = [psum.tile([P, 2 * C], F32, name="last_bank", tag=("d", "e")[u]) for u in range(2)]
+        first_banks = [psum.tile([P, C], F32, name="first_bank", tag=("f", "h")[u]) for u in range(2)]
+        for u in range(2):
+            layer1_turn(0, u, first_banks[u][:])
+        nc.vector.tensor_copy(hzero[:], first_banks[0][:])
+        nc.scalar.copy(hfront[:], first_banks[1][:, 0 : C // 2])
+        gate_on_scalar(1, *layer1_product(1, 0, H, "c"))
+        one_bank = psum.tile([P, C], F32, name="one_bank", tag="g")
+        late_bank = psum.tile([P, 3 * C], F32, name="late_bank", tag="e")
+        layer1_turn(1, 0, one_bank[:])
+        layer1_turn(1, 1, late_bank[:, 0:C])
+        nc.scalar.copy(hone[:], one_bank[:])
+        hback = keep.tile([P, C // 2], F32, name="hback", tag="hrow1", align_bytes=64)
+        nc.scalar.copy(hback[:], first_banks[1][:, C // 2 : C])
+        last_bank = psum.tile([P, 2 * C], F32, name="last_bank", tag="d")
         for e in range(2, E):
             layer1_gather(e)
             gate_on_scalar(e, *layer1_product(e, 0, H, ("b", "a")[e - 2]))
-            for u in range(2):
-                layer1_turn(e, u, last_banks[u][:, slots(e - 2)])
-        for u in range(2):
-            nc.scalar.copy(hlast[u][:], last_banks[u][:])
-        for e in range(2):
-            for u in range(2):
-                nc.vector.tensor_copy(ctok[u][:].indirect(list1[:, entries(e)]), hboth[e][:, slots(u)])
-        for u in range(2):
-            nc.vector.tensor_copy(ctok[u][:].indirect(list1[:, 2 * LIST_COLS :]), hlast[u][:])
+            layer1_turn(e, 0, last_bank[:, slots(e - 2)])
+            layer1_turn(e, 1, late_bank[:, slots(e - 1)])
+        nc.scalar.copy(hlast[:], last_bank[:])
+        nc.scalar.copy(hlate[:], late_bank[:])
+        half = LIST_COLS // 2
+        for u, first, last, words in (
+            (0, 0, LIST_COLS, hzero),
+            (1, 0, half, hfront),
+            (0, LIST_COLS, 2 * LIST_COLS, hone),
+            (1, half, LIST_COLS, hback),
+            (0, 2 * LIST_COLS, 4 * LIST_COLS, hlast),
+            (1, LIST_COLS, 4 * LIST_COLS, hlate),
+        ):
+            nc.vector.tensor_copy(ctok[u][:].indirect(list1[:, first:last]), words[:])
         w2b = [
-            keep.tile([P, 2, N, 4], BF16, name="w2b%d" % j, tag=tag, align_bytes=64)
-            for j, tag in enumerate(("hrow3", "w2b2"))
+            keep.tile([P, count, N, 4], BF16, name="w2b%d" % j, tag=tag, align_bytes=64)
+            for j, (count, tag) in enumerate(((1, "hrow3"), (1, "w2b1"), (2, "w2b2")))
         ]
-        for f in range(E):
-            w2_round(f, w2b[f // 2][:, f % 2])
+        w2_round(0, w2b[0][:, 0])
+        w2_round(1, w2b[1][:, 0])
+        w2_round(2, w2b[2][:, 0])
+        w2_round(3, w2b[2][:, 1])
+        cplane = [keep.tile([P, T], BF16, name="cplane%d" % d, tag=("cplane0", "w2raw3")[d], align_bytes=64) for d in range(2)]
         pairs = ctok[0][:].bitcast(BF16).rearrange("p (s d) -> p s d", d=2)
-        for d in range(2):
-            nc.scalar.copy(cplane[d][:], pairs[:, :, d])
+        nc.scalar.copy(cplane[0][:], pairs[:, :, 0])
+        gpsimd_round(cplane[1][:], pairs[:, :, 1])
 
         cs = keep.tile([P, T], U8, name="cs", align_bytes=64)
-        ycol = keep.tile([P, 2, T], F32, name="ycol", align_bytes=64)
-        otok = [keep.tile([P, (T, WIDE)[v]], F32, name="otok%d" % v, tag=("w2b2", "otok1")[v], align_bytes=64) for v in range(2)]
+        yfirst = keep.tile([P, 2, C], F32, name="yfirst", tag="yfirst", align_bytes=64)
+        yrest = keep.tile([P, 2, T - C], F32, name="yrest", align_bytes=64)
+        otok = [keep.tile([P, T], F32, name="otok%d" % v, tag=("w2b2", "otok1")[v], align_bytes=64) for v in range(2)]
 
         def layer2_product(f):
             cw = keep.tile([P, C], U32, name="cw%d" % f, tag="cw%d" % f, align_bytes=64)
@@ -219,20 +232,32 @@ def tile_moe_ser_none_kernel(tc, x_words, x_scales, w1_words, w1_scales, w2, gat
                 )
             return bank
 
-        for f in range(E):
-            layer2_gather(f)
-        for f in range(E):
-            if f < 3:
-                w2_quantise(f, (1, 1, 2)[f], ("hlast1", "cg0", "cg1")[f])
+        for pair in range(0, E, 2):
+            for d in range(2):
+                for f in (pair, pair + 1):
+                    layer2_gather_plane(f, d)
+            for f in (pair, pair + 1):
+                layer2_gather_words(f)
+        def layer2_scatter(sums, first, last):
+            for v in range(2):
+                nc.vector.tensor_tensor(
+                    otok[v][:].indirect(list2[:, first * LIST_COLS : (last + 1) * LIST_COLS]),
+                    sums[:, v, :],
+                    g2[:, first * C : (last + 1) * C],
+                    mybir.AluOpType.mult,
+                )
+
+        def layer2_expert(f):
             bank = layer2_product(f)
-            nc.scalar.copy(ycol[:, :, slots(f)], bank[:].rearrange("p (v s) -> p v s", v=2))
-        for v, first, last in PIECES:
-            cols = slice(first * C, (last + 1) * C)
-            nc.vector.tensor_tensor(
-                otok[v][:].indirect(list2[:, first * LIST_COLS : (last + 1) * LIST_COLS]),
-                ycol[:, v, cols],
-                g2[:, cols],
-                mybir.AluOpType.mult,
-            )
+            sums = yfirst[:] if f == 0 else yrest[:, :, slots(f - 1)]
+            nc.scalar.copy(sums, bank[:].rearrange("p (v s) -> p v s", v=2))
+
+        for f in range(E - 1):
+            w2_quantise(f, (1, 1, 2)[f], ("hlate", "cg0", "cg1")[f])
+            layer2_expert(f)
+        layer2_expert(3)
+        layer2_scatter(yfirst[:], 0, 0)
+        layer2_scatter(yrest[:, :, 0:C], 1, 1)
+        layer2_scatter(yrest[:, :, C:], 2, 3)
         for v in range(2):
-            nc.sync.dma_start(out[v * P : (v + 1) * P, :], otok[v][:, 0:T])
+            nc.sync.dma_start(out[v * P : (v + 1) * P, :], otok[v][:])

@@ -119,12 +119,20 @@ def tile_moe_ser_none_kernel(tc, x_words, x_scales, w1_words, w1_scales, w2, gat
             words = hrow[e][:].rearrange("s u p d -> s (u p d)").bitcast(F32)
             nc.tensor.transpose(bank, words[:, u * P : (u + 1) * P], ident[:])
 
+        cpair = [keep.tile([P, 2, C, 2], BF16, name="cpair%d" % f, align_bytes=64) for f in range(E)]
+
         def layer2_gather_plane(f, d):
-            nc.scalar.activation(out=cg[f][:, :, d], in_=cplane[d][:].indirect(list2[:, entries(f)]), func=COPY)
+            nc.scalar.activation(out=cpair[f][:, 0, :, d], in_=cplane[d][:].indirect(list2[:, entries(f)]), func=COPY)
 
         def layer2_gather_words(f):
-            words = cg[f][:].rearrange("p s t -> p (s t)").bitcast(U32).rearrange("p (s u) -> p s u", u=2)
-            nc.vector.tensor_copy(words[:, :, 1], ctok[1][:, 0:T].bitcast(U32).indirect(list2[:, entries(f)]))
+            words = cpair[f][:, 1].rearrange("p s d -> p (s d)").bitcast(U32)
+            nc.vector.tensor_copy(words, ctok[1][:].bitcast(U32).indirect(list2[:, entries(f)]))
+
+        def layer2_weave(f):
+            nc.scalar.copy(
+                cg[f][:].rearrange("p s t -> p (s t)").bitcast(F32).rearrange("p (s u) -> p s u", u=2),
+                cpair[f][:].rearrange("p u s d -> p (u s d)").bitcast(F32).rearrange("p (u s) -> p s u", u=2),
+            )
 
         w2w = []
         w2s = keep.tile([P, E, N], U8, name="w2s", align_bytes=64)
@@ -207,6 +215,7 @@ def tile_moe_ser_none_kernel(tc, x_words, x_scales, w1_words, w1_scales, w2, gat
         nc.scalar.copy(cplane[0][:], pairs[:, :, 0])
         gpsimd_round(cplane[1][:], pairs[:, :, 1])
 
+        w2_quantise(0, 1, "hlate")
         cs = keep.tile([P, T], U8, name="cs", align_bytes=64)
         yfirst = keep.tile([P, 2, C], F32, name="yfirst", tag="yfirst", align_bytes=64)
         yrest = keep.tile([P, 2, T - C], F32, name="yrest", align_bytes=64)
@@ -232,12 +241,16 @@ def tile_moe_ser_none_kernel(tc, x_words, x_scales, w1_words, w1_scales, w2, gat
                 )
             return bank
 
-        for pair in range(0, E, 2):
-            for d in range(2):
-                for f in (pair, pair + 1):
-                    layer2_gather_plane(f, d)
-            for f in (pair, pair + 1):
-                layer2_gather_words(f)
+        for f in range(E):
+            layer2_gather_words(f)
+        for d in range(2):
+            for f in range(2):
+                layer2_gather_plane(f, d)
+        for d in range(2):
+            for f in range(2, E):
+                layer2_gather_plane(f, d)
+            for f in range(2):
+                layer2_weave(2 * d + f)
         def layer2_scatter(sums, first, last):
             for v in range(2):
                 nc.vector.tensor_tensor(
@@ -253,7 +266,8 @@ def tile_moe_ser_none_kernel(tc, x_words, x_scales, w1_words, w1_scales, w2, gat
             nc.scalar.copy(sums, bank[:].rearrange("p (v s) -> p v s", v=2))
 
         for f in range(E - 1):
-            w2_quantise(f, (1, 1, 2)[f], ("hlate", "cg0", "cg1")[f])
+            if f > 0:
+                w2_quantise(f, (1, 1, 2)[f], ("hlate", "cg0", "cg1")[f])
             layer2_expert(f)
         layer2_expert(3)
         layer2_scatter(yfirst[:], 0, 0)

@@ -52,9 +52,9 @@ def tile_moe_ser_none_kernel(tc, x_words, x_scales, w1_words, w1_scales, w2, gat
         w1s_rows = w1_scales[:, 0].rearrange("e (q r) n -> r q e n", r=4)
         make_identity(nc, ident[:])
         nc.sync.dma_start(list1[:], offs)
+        nc.sync.dma_start(xw[:], x_words[0].rearrange("p t d -> p (t d)").bitcast(I32))
         for r in range(4):
             nc.sync.dma_start(xs[r:P:32, :].bitcast(I32), xs_rows[r].bitcast(I32))
-        nc.sync.dma_start(xw[:], x_words[0].rearrange("p t d -> p (t d)").bitcast(I32))
         nc.sync.dma_start(g1rows[:], gate1[0:32, :].rearrange("r (e c) -> (r e) c", c=C))
         nc.sync.dma_start(w1first[:].bitcast(I32), w1_words[0, 0].bitcast(I32))
         for r in range(4):

@@ -46,6 +46,7 @@ def tile_moe_ser_none_kernel(tc, x_words, x_scales, w1_words, w1_scales, w2, gat
         ident = keep.tile([P, P], F32, name="ident")
 
         nc.gpsimd.memset(xs[:].bitcast(I32), 0)
+        nc.gpsimd.memset(g1rows[:], 0.0)
         nc.vector.memset(w1s[:].rearrange("p e n -> p (e n)").bitcast(I32), 0)
 
         xs_rows = x_scales[0].rearrange("(q r) n -> r q n", r=4)
@@ -55,7 +56,7 @@ def tile_moe_ser_none_kernel(tc, x_words, x_scales, w1_words, w1_scales, w2, gat
         nc.sync.dma_start(xw[:], x_words[0].rearrange("p t d -> p (t d)").bitcast(I32))
         for r in range(4):
             nc.sync.dma_start(xs[r:P:32, :].bitcast(I32), xs_rows[r].bitcast(I32))
-        nc.sync.dma_start(g1rows[:], gate1[0:32, :].rearrange("r (e c) -> (r e) c", c=C))
+        nc.sync.dma_start(g1rows[0:E, :], gate1[0].rearrange("(e c) -> e c", c=C))
         nc.sync.dma_start(w1first[:].bitcast(I32), w1_words[0, 0].bitcast(I32))
         for r in range(4):
             nc.sync.dma_start(w1s[r:P:32, :, :].bitcast(I32), w1s_rows[r].bitcast(I32))

@@ -28,6 +28,7 @@ def tile_moe_ser_none_kernel(tc, x_words, x_scales, w1_words, w1_scales, w2, gat
     nc = tc.nc
     with ExitStack() as ctx:
         keep = ctx.enter_context(tc.tile_pool(name="keep", bufs=1))
+        reuse = ctx.enter_context(tc.tile_pool(name="reuse", bufs=1))
         psum = ctx.enter_context(tc.psum_pool(name="psum", bufs=1))
 
         def slots(e):
@@ -87,10 +88,10 @@ def tile_moe_ser_none_kernel(tc, x_words, x_scales, w1_words, w1_scales, w2, gat
         hzero = keep.tile([P, C], F32, name="hzero", align_bytes=64)
         hfront = keep.tile([P, C // 2], F32, name="hfront", align_bytes=64)
         hone = keep.tile([P, C], F32, name="hone", align_bytes=64)
-        hlast = keep.tile([P, 2 * C], F32, name="hlast", align_bytes=64)
+        hlast = keep.tile([P, 2 * C], F32, name="hlast", tag="hlast", align_bytes=64)
         hlate = keep.tile([P, 3 * C], F32, name="hlate", tag="hlate", align_bytes=64)
         ctok = [keep.tile([P, T], F32, name="ctok%d" % u, align_bytes=64) for u in range(2)]
-        cg = [keep.tile([P, C, 4], BF16, name="cg%d" % f, tag="cg%d" % f, align_bytes=64) for f in range(E)]
+        cg = [keep.tile([P, C, 4], BF16, name="cg%d" % f, tag="cg%d" % f, align_bytes=64)[:] for f in range(2)]
 
         def layer1_gather(e):
             xgw.append(keep.tile([P, C], U32, name="xgw%d" % e, tag="xgw%d" % (e % 3), align_bytes=64))
@@ -120,7 +121,8 @@ def tile_moe_ser_none_kernel(tc, x_words, x_scales, w1_words, w1_scales, w2, gat
             words = hrow[e][:].rearrange("s u p d -> s (u p d)").bitcast(F32)
             nc.tensor.transpose(bank, words[:, u * P : (u + 1) * P], ident[:])
 
-        cpair = [keep.tile([P, 2, C, 2], BF16, name="cpair%d" % f, align_bytes=64) for f in range(E)]
+        cpair = [keep.tile([P, 2, C, 2], BF16, name="cpair%d" % f, align_bytes=64) for f in (0, 2, 3)]
+        cpair[1:1] = [reuse.tile([P, 2, C, 2], BF16, name="cpair1", offset=1024, align_bytes=64)]
 
         def layer2_gather_plane(f, d):
             nc.scalar.activation(out=cpair[f][:, 0, :, d], in_=cplane[d][:].indirect(list2[:, entries(f)]), func=COPY)
@@ -131,7 +133,7 @@ def tile_moe_ser_none_kernel(tc, x_words, x_scales, w1_words, w1_scales, w2, gat
 
         def layer2_weave(f):
             nc.scalar.copy(
-                cg[f][:].rearrange("p s t -> p (s t)").bitcast(F32).rearrange("p (s u) -> p s u", u=2),
+                cg[f].rearrange("p s t -> p (s t)").bitcast(F32).rearrange("p (s u) -> p s u", u=2),
                 cpair[f][:].rearrange("p u s d -> p (u s d)").bitcast(F32).rearrange("p (u s) -> p s u", u=2),
             )
 
@@ -157,8 +159,7 @@ def tile_moe_ser_none_kernel(tc, x_words, x_scales, w1_words, w1_scales, w2, gat
             else:
                 gpsimd_round(rounded, w2raw[f].rearrange("p t n -> p n t"))
 
-        def w2_quantise(first, count, tag):
-            codes = keep.tile([P, count * N], U32, name="w2w%d" % first, tag=tag, align_bytes=64)
+        def w2_quantise(first, count, codes):
             w2w.extend(codes[:, j * N : (j + 1) * N] for j in range(count))
             nc.vector.quantize_mx(
                 out=codes[:].bitcast(FP8X4),
@@ -216,63 +217,72 @@ def tile_moe_ser_none_kernel(tc, x_words, x_scales, w1_words, w1_scales, w2, gat
         nc.scalar.copy(cplane[0][:], pairs[:, :, 0])
         gpsimd_round(cplane[1][:], pairs[:, :, 1])
 
-        w2_quantise(0, 1, "hlate")
+        w2_quantise(0, 1, keep.tile([P, N], U32, name="w2w0", tag="hlast", align_bytes=64))
         cs = keep.tile([P, T], U8, name="cs", align_bytes=64)
-        yfirst = keep.tile([P, 2, C], F32, name="yfirst", tag="yfirst", align_bytes=64)
-        yrest = keep.tile([P, 2, T - C], F32, name="yrest", align_bytes=64)
-        otok = [keep.tile([P, T], F32, name="otok%d" % v, tag=("w2b2", "otok1")[v], align_bytes=64) for v in range(2)]
+        otok = [keep.tile([P, T], F32, name="otok%d" % v, align_bytes=64) for v in range(2)]
 
-        def layer2_product(f):
-            cw = keep.tile([P, C], U32, name="cw%d" % f, tag="cw%d" % f, align_bytes=64)
+        def c_quantise(first, values, cw):
+            count = values.shape[1] // C
             nc.vector.quantize_mx(
                 out=cw[:].bitcast(FP8X4),
-                scales=cs[:, slots(f)],
-                in_=cg[f][:].rearrange("p s t -> p (s t)"),
+                scales=cs[:, first * C : (first + count) * C],
+                in_=values.rearrange("p s t -> p (s t)"),
             )
-            bank = psum.tile([P, 2 * C], F32, name="y_bank", tag=("a", "b", "c", "d")[f])
-            for v in range(2):
-                nc.tensor.matmul_mx(
-                    out=bank[:, v * C : (v + 1) * C],
-                    lhsT=w2w[f][:, v * P : (v + 1) * P].bitcast(FP8X4),
-                    lhsT_scale=w2s[:, f, v * P : (v + 1) * P],
-                    rhs=cw[:].bitcast(FP8X4),
-                    rhs_scale=cs[:, slots(f)],
-                    start=True,
-                    stop=True,
-                )
-            return bank
+            return cw
+
+        def layer2_product(f, v, codes, sums):
+            nc.tensor.matmul_mx(
+                out=sums,
+                lhsT=w2w[f][:, v * P : (v + 1) * P].bitcast(FP8X4),
+                lhsT_scale=w2s[:, f, v * P : (v + 1) * P],
+                rhs=codes.bitcast(FP8X4),
+                rhs_scale=cs[:, slots(f)],
+                start=True,
+                stop=True,
+            )
+
+        def layer2_sums(pieces, codes, first, letter):
+            bank = psum.tile([P, len(pieces) * C], F32, name="y_bank", tag=letter)
+            for j, (f, v) in enumerate(pieces):
+                layer2_product(f, v, codes[:, slots(f - first)], bank[:, slots(j)])
+            sums = keep.tile([P, len(pieces) * C], F32, name="ysums" + letter, tag="ysums" + letter, align_bytes=64)
+            nc.scalar.copy(sums[:], bank[:])
+            return sums
+
+        def layer2_scatter(v, sums, first, last):
+            nc.vector.tensor_tensor(
+                otok[v][:].indirect(list2[:, first * LIST_COLS : (last + 1) * LIST_COLS]),
+                sums,
+                g2[:, first * C : (last + 1) * C],
+                mybir.AluOpType.mult,
+            )
 
         for f in range(E):
             layer2_gather_words(f)
         for d in range(2):
             for f in range(2):
                 layer2_gather_plane(f, d)
-        for d in range(2):
-            for f in range(2, E):
-                layer2_gather_plane(f, d)
-            for f in range(2):
-                layer2_weave(2 * d + f)
-        def layer2_scatter(sums, first, last):
-            for v in range(2):
-                nc.vector.tensor_tensor(
-                    otok[v][:].indirect(list2[:, first * LIST_COLS : (last + 1) * LIST_COLS]),
-                    sums[:, v, :],
-                    g2[:, first * C : (last + 1) * C],
-                    mybir.AluOpType.mult,
-                )
-
-        def layer2_expert(f):
-            bank = layer2_product(f)
-            sums = yfirst[:] if f == 0 else yrest[:, :, slots(f - 1)]
-            nc.scalar.copy(sums, bank[:].rearrange("p (v s) -> p v s", v=2))
-
-        for f in range(E - 1):
-            if f > 0:
-                w2_quantise(f, (1, 1, 2)[f], ("hlate", "cg0", "cg1")[f])
-            layer2_expert(f)
-        layer2_expert(3)
-        layer2_scatter(yfirst[:], 0, 0)
-        layer2_scatter(yrest[:, :, 0:C], 1, 1)
-        layer2_scatter(yrest[:, :, C:], 2, 3)
+        for f in range(2, E):
+            layer2_gather_plane(f, 0)
+        for f in range(2):
+            layer2_weave(f)
+        for f in range(2, E):
+            layer2_gather_plane(f, 1)
+        cw = c_quantise(0, cg[0], keep.tile([P, C], U32, name="cw0", tag="cw0", align_bytes=64))
+        first_sums = [layer2_sums([(0, v)], cw, 0, "ab"[v]) for v in range(2)]
+        cglate = keep.tile([P, 2 * C, 4], BF16, name="cglate", tag="cw0", align_bytes=64)
+        cg.extend(cglate[:, slots(j), :] for j in range(2))
+        for f in range(2, E):
+            layer2_weave(f)
+        w2_quantise(1, 1, reuse.tile([P, N], U32, name="w2w1", offset=64, align_bytes=64))
+        second_sums = layer2_sums([(1, 0), (1, 1)], c_quantise(1, cg[1], keep.tile([P, C], U32, name="cw1", align_bytes=64)), 1, "c")
+        w2_quantise(2, 2, reuse.tile([P, 2 * N], U32, name="w2w2", offset=1984, align_bytes=64))
+        for v in range(2):
+            layer2_scatter(v, first_sums[v][:], 0, 0)
+        cw = c_quantise(2, cglate[:], keep.tile([P, 2 * C], U32, name="cw2", align_bytes=64))
+        for v in range(2):
+            layer2_scatter(v, second_sums[:, slots(v)], 1, 1)
+        for v in range(2):
+            layer2_scatter(v, layer2_sums([(2, v), (3, v)], cw, 2, "de"[v])[:], 2, 3)
         for v in range(2):
             nc.sync.dma_start(out[v * P : (v + 1) * P, :], otok[v][:])

@@ -91,7 +91,9 @@ def tile_moe_ser_none_kernel(tc, x_words, x_scales, w1_words, w1_scales, w2, gat
         hlast = keep.tile([P, 2 * C], F32, name="hlast", tag="hlast", align_bytes=64)
         hlate = keep.tile([P, 3 * C], F32, name="hlate", tag="hlate", align_bytes=64)
         ctok = [keep.tile([P, T], F32, name="ctok%d" % u, align_bytes=64) for u in range(2)]
-        cg = [keep.tile([P, C, 4], BF16, name="cg%d" % f, tag="cg%d" % f, align_bytes=64)[:] for f in range(2)]
+        cgmid = keep.tile([P, 2 * C, 4], BF16, name="cgmid", align_bytes=64)
+        cg = [keep.tile([P, C, 4], BF16, name="cg%d" % f, align_bytes=64)[:] for f in (0, 3)]
+        cg[1:1] = [cgmid[:, slots(j), :] for j in range(2)]
 
         def layer1_gather(e):
             xgw.append(keep.tile([P, C], U32, name="xgw%d" % e, tag="xgw%d" % (e % 3), align_bytes=64))
@@ -121,8 +123,9 @@ def tile_moe_ser_none_kernel(tc, x_words, x_scales, w1_words, w1_scales, w2, gat
             words = hrow[e][:].rearrange("s u p d -> s (u p d)").bitcast(F32)
             nc.tensor.transpose(bank, words[:, u * P : (u + 1) * P], ident[:])
 
-        cpair = [keep.tile([P, 2, C, 2], BF16, name="cpair%d" % f, align_bytes=64) for f in (0, 2, 3)]
+        cpair = [keep.tile([P, 2, C, 2], BF16, name="cpair%d" % f, align_bytes=64) for f in (0, 2)]
         cpair[1:1] = [reuse.tile([P, 2, C, 2], BF16, name="cpair1", offset=1024, align_bytes=64)]
+        cpair.append(reuse.tile([P, 2, C, 2], BF16, name="cpair3", offset=6592, align_bytes=64))
 
         def layer2_gather_plane(f, d):
             nc.scalar.activation(out=cpair[f][:, 0, :, d], in_=cplane[d][:].indirect(list2[:, entries(f)]), func=COPY)
@@ -150,14 +153,11 @@ def tile_moe_ser_none_kernel(tc, x_words, x_scales, w1_words, w1_scales, w2, gat
                 op1=mybir.AluOpType.add,
             )
 
-        def w2_round(f, rounded):
-            if f == 0:
-                nc.scalar.copy(
-                    rounded.rearrange("p (c i) t -> p c t i", i=4),
-                    w2raw[f].rearrange("p t (c i) -> p c t i", i=4),
-                )
-            else:
-                gpsimd_round(rounded, w2raw[f].rearrange("p t n -> p n t"))
+        def scalar_round(rounded, values):
+            nc.scalar.copy(
+                rounded.rearrange("p (c i) t -> p c t i", i=4),
+                values.rearrange("p t (c i) -> p c t i", i=4),
+            )
 
         def w2_quantise(first, count, codes):
             w2w.extend(codes[:, j * N : (j + 1) * N] for j in range(count))
@@ -204,15 +204,14 @@ def tile_moe_ser_none_kernel(tc, x_words, x_scales, w1_words, w1_scales, w2, gat
             (1, LIST_COLS, 4 * LIST_COLS, hlate),
         ):
             nc.vector.tensor_copy(ctok[u][:].indirect(list1[:, first:last]), words[:])
-        w2b = [
-            keep.tile([P, count, N, 4], BF16, name="w2b%d" % j, tag=tag, align_bytes=64)
-            for j, (count, tag) in enumerate(((1, "hrow3"), (1, "w2b1"), (2, "w2b2")))
-        ]
-        w2_round(0, w2b[0][:, 0])
-        w2_round(1, w2b[1][:, 0])
-        w2_round(2, w2b[2][:, 0])
-        w2_round(3, w2b[2][:, 1])
-        cplane = [keep.tile([P, T], BF16, name="cplane%d" % d, tag=("cplane0", "w2raw3")[d], align_bytes=64) for d in range(2)]
+        w2b = {
+            0: keep.tile([P, 1, N, 4], BF16, name="w2b0", tag="hrow3", align_bytes=64),
+            1: keep.tile([P, 2, N, 4], BF16, name="w2b1", align_bytes=64),
+        }
+        scalar_round(w2b[0][:, 0], w2raw[0])
+        for f in (1, 2):
+            gpsimd_round(w2b[1][:, f - 1], w2raw[f].rearrange("p t n -> p n t"))
+        cplane = [keep.tile([P, T], BF16, name="cplane%d" % d, tag=("cplane0", "w2raw2")[d], align_bytes=64) for d in range(2)]
         pairs = ctok[0][:].bitcast(BF16).rearrange("p (s d) -> p s d", d=2)
         nc.scalar.copy(cplane[0][:], pairs[:, :, 0])
         gpsimd_round(cplane[1][:], pairs[:, :, 1])
@@ -241,13 +240,19 @@ def tile_moe_ser_none_kernel(tc, x_words, x_scales, w1_words, w1_scales, w2, gat
                 stop=True,
             )
 
-        def layer2_sums(pieces, codes, first, letter):
+        def layer2_products(pieces, codes, first, letter):
             bank = psum.tile([P, len(pieces) * C], F32, name="y_bank", tag=letter)
             for j, (f, v) in enumerate(pieces):
                 layer2_product(f, v, codes[:, slots(f - first)], bank[:, slots(j)])
-            sums = keep.tile([P, len(pieces) * C], F32, name="ysums" + letter, tag="ysums" + letter, align_bytes=64)
+            return bank
+
+        def layer2_copy(bank, letter):
+            sums = keep.tile([P, bank[:].shape[1]], F32, name="ysums" + letter, tag="w2raw3" if letter == "d" else "ysums" + letter, align_bytes=64)
             nc.scalar.copy(sums[:], bank[:])
             return sums
+
+        def layer2_sums(pieces, codes, first, letter):
+            return layer2_copy(layer2_products(pieces, codes, first, letter), letter)
 
         def layer2_scatter(v, sums, first, last):
             nc.vector.tensor_tensor(
@@ -257,32 +262,35 @@ def tile_moe_ser_none_kernel(tc, x_words, x_scales, w1_words, w1_scales, w2, gat
                 mybir.AluOpType.mult,
             )
 
-        for f in range(E):
+        for f in range(E - 1):
             layer2_gather_words(f)
         for d in range(2):
             for f in range(2):
                 layer2_gather_plane(f, d)
-        for f in range(2, E):
-            layer2_gather_plane(f, 0)
-        for f in range(2):
+        for d in range(2):
+            layer2_gather_plane(2, d)
+        for f in range(E - 1):
             layer2_weave(f)
-        for f in range(2, E):
-            layer2_gather_plane(f, 1)
-        cw = c_quantise(0, cg[0], keep.tile([P, C], U32, name="cw0", tag="cw0", align_bytes=64))
+        cw = c_quantise(0, cg[0], reuse.tile([P, C], U32, name="cw0", offset=6144, align_bytes=64))
         first_sums = [layer2_sums([(0, v)], cw, 0, "ab"[v]) for v in range(2)]
-        cglate = keep.tile([P, 2 * C, 4], BF16, name="cglate", tag="cw0", align_bytes=64)
-        cg.extend(cglate[:, slots(j), :] for j in range(2))
-        for f in range(2, E):
-            layer2_weave(f)
-        w2_quantise(1, 1, reuse.tile([P, N], U32, name="w2w1", offset=64, align_bytes=64))
-        second_sums = layer2_sums([(1, 0), (1, 1)], c_quantise(1, cg[1], keep.tile([P, C], U32, name="cw1", align_bytes=64)), 1, "c")
-        w2_quantise(2, 2, reuse.tile([P, 2 * N], U32, name="w2w2", offset=1984, align_bytes=64))
+        w2_quantise(1, 2, reuse.tile([P, 2 * N], U32, name="w2w1", offset=1984, align_bytes=64))
+        cw = c_quantise(1, cgmid[:], keep.tile([P, 2 * C], U32, name="cw1", tag="cw1", align_bytes=64))
+        layer2_gather_words(3)
+        for d in range(2):
+            layer2_gather_plane(3, d)
+        layer2_weave(3)
+        banks = [layer2_products([(1, v), (2, v)], cw, 1, "cd"[v]) for v in range(2)]
+        middle_sums = [layer2_copy(banks[0], "c")]
+        w2b[3] = keep.tile([P, 1, N, 4], BF16, name="w2b3", tag="cw1", align_bytes=64)
+        scalar_round(w2b[3][:, 0], w2raw[3])
+        middle_sums.append(layer2_copy(banks[1], "d"))
         for v in range(2):
             layer2_scatter(v, first_sums[v][:], 0, 0)
-        cw = c_quantise(2, cglate[:], keep.tile([P, 2 * C], U32, name="cw2", align_bytes=64))
+        layer2_scatter(0, middle_sums[0][:], 1, 2)
+        cw = c_quantise(3, cg[3], keep.tile([P, C], U32, name="cw3", tag="ysumsa", align_bytes=64))
+        w2_quantise(3, 1, keep.tile([P, N], U32, name="w2w3", align_bytes=64))
+        layer2_scatter(1, middle_sums[1][:], 1, 2)
         for v in range(2):
-            layer2_scatter(v, second_sums[:, slots(v)], 1, 1)
-        for v in range(2):
-            layer2_scatter(v, layer2_sums([(2, v), (3, v)], cw, 2, "de"[v])[:], 2, 3)
+            layer2_scatter(v, layer2_sums([(3, v)], cw, 3, "ef"[v])[:], 3, 3)
         for v in range(2):
             nc.sync.dma_start(out[v * P : (v + 1) * P, :], otok[v][:])

@@ -182,7 +182,6 @@ def tile_moe_ser_none_kernel(tc, x_words, x_scales, w1_words, w1_scales, w2, gat
         one_bank = psum.tile([P, C], F32, name="one_bank", tag="g")
         late_bank = psum.tile([P, 3 * C], F32, name="late_bank", tag="e")
         layer1_turn(1, 0, one_bank[:])
-        layer1_turn(1, 1, late_bank[:, 0:C])
         nc.scalar.copy(hone[:], one_bank[:])
         hback = keep.tile([P, C // 2], F32, name="hback", tag="hrow1", align_bytes=64)
         nc.scalar.copy(hback[:], first_banks[1][:, C // 2 : C])
@@ -191,8 +190,9 @@ def tile_moe_ser_none_kernel(tc, x_words, x_scales, w1_words, w1_scales, w2, gat
             layer1_gather(e)
             gate_on_scalar(e, *layer1_product(e, 0, H, ("b", "a")[e - 2]))
             layer1_turn(e, 0, last_bank[:, slots(e - 2)])
-            layer1_turn(e, 1, late_bank[:, slots(e - 1)])
         nc.scalar.copy(hlast[:], last_bank[:])
+        for e in range(1, E):
+            layer1_turn(e, 1, late_bank[:, slots(e - 1)])
         nc.scalar.copy(hlate[:], late_bank[:])
         half = LIST_COLS // 2
         for u, first, last, words in (

@@ -168,11 +168,12 @@ def tile_moe_ser_none_kernel(tc, x_words, x_scales, w1_words, w1_scales, w2, gat
             )
 
         layer1_gather(0)
-        low = layer1_product(0, 0, H // 2, "a")
         high = layer1_product(0, H // 2, H // 2, "b")
+        quarters = [layer1_product(0, j * H // 4, H // 4, "ad"[j]) for j in range(2)]
         layer1_gather(1)
-        gate_on_vector(0, *low)
         gate_on_scalar(0, *high)
+        for quarter in quarters:
+            gate_on_vector(0, *quarter)
         first_banks = [psum.tile([P, C], F32, name="first_bank", tag=("f", "h")[u]) for u in range(2)]
         for u in range(2):
             layer1_turn(0, u, first_banks[u][:])

@@ -41,7 +41,7 @@ def tile_moe_ser_none_kernel(tc, x_words, x_scales, w1_words, w1_scales, w2, gat
         list2 = keep.tile([P, T // 16], U16, name="list2")
         xw = keep.tile([P, T], I32, name="xw", align_bytes=64)
         xs = keep.tile([P, T], U8, name="xs", align_bytes=64)
-        w1first = keep.tile([P, 2 * H], U8, name="w1first", align_bytes=64)
+        w1pair = [keep.tile([P, 2, 2 * H], U8, name="w1pair%d" % j, align_bytes=64) for j in range(2)]
         w1s = keep.tile([P, E, H], U8, name="w1s", align_bytes=64)
         g1rows = keep.tile([P, C], F32, name="g1rows", align_bytes=64)
         ident = keep.tile([P, P], F32, name="ident")
@@ -58,13 +58,11 @@ def tile_moe_ser_none_kernel(tc, x_words, x_scales, w1_words, w1_scales, w2, gat
         for r in range(4):
             nc.sync.dma_start(xs[r:P:32, :].bitcast(I32), xs_rows[r].bitcast(I32))
         nc.sync.dma_start(g1rows[0:E, :], gate1[0].rearrange("(e c) -> e c", c=C))
-        nc.sync.dma_start(w1first[:].bitcast(I32), w1_words[0, 0].bitcast(I32))
+        nc.sync.dma_start(w1pair[0][:].bitcast(I32), w1_words[0:2, 0].rearrange("e p n -> p e n").bitcast(I32))
         for r in range(4):
             nc.sync.dma_start(w1s[r:P:32, :, :].bitcast(I32), w1s_rows[r].bitcast(I32))
-        w1rest = keep.tile([P, E - 1, 2 * H], U8, name="w1rest", align_bytes=64)
-        nc.sync.dma_start(w1rest[:, 0, :].bitcast(I32), w1_words[1, 0].bitcast(I32))
-        nc.sync.dma_start(w1rest[:, 1:3, :].bitcast(I32), w1_words[2:4, 0].rearrange("e p n -> p e n").bitcast(I32))
-        w1w = [w1first[:]] + [w1rest[:, e, :] for e in range(E - 1)]
+        nc.sync.dma_start(w1pair[1][:].bitcast(I32), w1_words[2:4, 0].rearrange("e p n -> p e n").bitcast(I32))
+        w1w = [w1pair[e // 2][:, e % 2, :] for e in range(E)]
         nc.sync.dma_start(list2[:], offs2)
 
         def gate_columns(rows, name):

@@ -76,7 +76,7 @@ def tile_moe_ser_none_kernel(tc, x_words, x_scales, w1_words, w1_scales, w2, gat
 
         w2raw = [keep.tile([P, 4, N], F32, name="w2raw%d" % f, tag="w2raw%d" % f, align_bytes=64)[:] for f in range(E)]
         g2 = keep.tile([P, T], F32, name="g2", align_bytes=64)[:]
-        for f in range(E):
+        for f in (1, 0, 2, 3):
             nc.sync.dma_start(w2raw[f], w2[f].rearrange("(p j) n -> p j n", j=4))
         nc.sync.dma_start(g2, gate2)
 

@@ -12,6 +12,7 @@ U8 = mybir.dt.uint8
 FP8X4 = mybir.dt.float8_e4m3fn_x4
 FP4X4 = mybir.dt.float4_e2m1fn_x4
 COPY = mybir.ActivationFunctionType.Copy
+MULT = mybir.AluOpType.mult
 
 P = 128
 T = 512
@@ -28,7 +29,6 @@ def tile_moe_ser_none_kernel(tc, x_words, x_scales, w1_words, w1_scales, w2, gat
     nc = tc.nc
     with ExitStack() as ctx:
         keep = ctx.enter_context(tc.tile_pool(name="keep", bufs=1))
-        reuse = ctx.enter_context(tc.tile_pool(name="reuse", bufs=1))
         psum = ctx.enter_context(tc.psum_pool(name="psum", bufs=1))
 
         def slots(e):
@@ -89,9 +89,6 @@ def tile_moe_ser_none_kernel(tc, x_words, x_scales, w1_words, w1_scales, w2, gat
         hlast = keep.tile([P, 2 * C], F32, name="hlast", tag="hlast", align_bytes=64)
         hlate = keep.tile([P, 3 * C], F32, name="hlate", tag="hlate", align_bytes=64)
         ctok = [keep.tile([P, T], F32, name="ctok%d" % u, align_bytes=64) for u in range(2)]
-        cgmid = keep.tile([P, 2 * C, 4], BF16, name="cgmid", align_bytes=64)
-        cg = [keep.tile([P, C, 4], BF16, name="cg%d" % f, align_bytes=64)[:] for f in (0, 3)]
-        cg[1:1] = [cgmid[:, slots(j), :] for j in range(2)]
 
         def layer1_gather(e):
             xgw.append(keep.tile([P, C], U32, name="xgw%d" % e, tag="xgw%d" % (e % 3), align_bytes=64))
@@ -121,26 +118,6 @@ def tile_moe_ser_none_kernel(tc, x_words, x_scales, w1_words, w1_scales, w2, gat
             words = hrow[e][:].rearrange("s u p d -> s (u p d)").bitcast(F32)
             nc.tensor.transpose(bank, words[:, u * P : (u + 1) * P], ident[:])
 
-        cpair = [keep.tile([P, 2, C, 2], BF16, name="cpair%d" % f, align_bytes=64) for f in (0, 2)]
-        cpair[1:1] = [reuse.tile([P, 2, C, 2], BF16, name="cpair1", offset=1024, align_bytes=64)]
-        cpair.append(reuse.tile([P, 2, C, 2], BF16, name="cpair3", offset=6592, align_bytes=64))
-
-        def layer2_gather_plane(f, d):
-            nc.scalar.activation(out=cpair[f][:, 0, :, d], in_=cplane[d][:].indirect(list2[:, entries(f)]), func=COPY)
-
-        def layer2_gather_words(f):
-            words = cpair[f][:, 1].rearrange("p s d -> p (s d)").bitcast(U32)
-            nc.vector.tensor_copy(words, ctok[1][:].bitcast(U32).indirect(list2[:, entries(f)]))
-
-        def layer2_weave(f):
-            nc.scalar.copy(
-                cg[f].rearrange("p s t -> p (s t)").bitcast(F32).rearrange("p (s u) -> p s u", u=2),
-                cpair[f][:].rearrange("p u s d -> p (u s d)").bitcast(F32).rearrange("p (u s) -> p s u", u=2),
-            )
-
-        w2w = []
-        w2s = keep.tile([P, E, N], U8, name="w2s", align_bytes=64)
-
         def gpsimd_round(rounded, values):
             nc.gpsimd.tensor_scalar(
                 out=rounded,
@@ -155,14 +132,6 @@ def tile_moe_ser_none_kernel(tc, x_words, x_scales, w1_words, w1_scales, w2, gat
             nc.scalar.copy(
                 rounded.rearrange("p (c i) t -> p c t i", i=4),
                 values.rearrange("p t (c i) -> p c t i", i=4),
-            )
-
-        def w2_quantise(first, count, codes):
-            w2w.extend(codes[:, j * N : (j + 1) * N] for j in range(count))
-            nc.vector.quantize_mx(
-                out=codes[:].bitcast(FP8X4),
-                scales=w2s[:, first : first + count, :].rearrange("p f n -> p (f n)"),
-                in_=w2b[first][:].rearrange("p f n t -> p (f n t)"),
             )
 
         layer1_gather(0)
@@ -215,81 +184,117 @@ def tile_moe_ser_none_kernel(tc, x_words, x_scales, w1_words, w1_scales, w2, gat
         nc.scalar.copy(cplane[0][:], pairs[:, :, 0])
         gpsimd_round(cplane[1][:], pairs[:, :, 1])
 
-        w2_quantise(0, 1, keep.tile([P, N], U32, name="w2w0", tag="hlast", align_bytes=64))
-        cs = keep.tile([P, T], U8, name="cs", align_bytes=64)
-        otok = [keep.tile([P, T], F32, name="otok%d" % v, align_bytes=64) for v in range(2)]
+        def sbuf(shape, dtype, name, tag=None):
+            return keep.tile(shape, dtype, name=name, tag=tag or name, align_bytes=64)
 
-        def c_quantise(first, values, cw):
-            count = values.shape[1] // C
+        def span(first, count):
+            return slice(first * C, (first + count) * C)
+
+        def list_span(first, count):
+            return slice(first * LIST_COLS, (first + count) * LIST_COLS)
+
+        def interleave(copy, rounded, values):
+            copy(rounded.rearrange("p (c i) t -> p c t i", i=4), values.rearrange("p t (c i) -> p c t i", i=4))
+
+        cpair = [sbuf([P, 2, C, 2], BF16, "cpair%d" % f) for f in range(E)]
+        cgmid = sbuf([P, 2 * C, 4], BF16, "cgmid")
+        cg = [sbuf([P, C, 4], BF16, "cg0")[:], cgmid[:, slots(0), :], cgmid[:, slots(1), :], sbuf([P, C, 4], BF16, "cg3")[:]]
+        w2s = sbuf([P, E, N], U8, "w2s")
+        cs = sbuf([P, T], U8, "cs")
+        otok = [sbuf([P, T], F32, "otok%d" % v) for v in range(2)]
+        w2w = {}
+
+        def gather_plane(f, d):
+            nc.scalar.activation(out=cpair[f][:, 0, :, d], in_=cplane[d][:].indirect(list2[:, entries(f)]), func=COPY)
+
+        def gather_pair(f):
+            words = cpair[f][:, 1].rearrange("p s d -> p (s d)").bitcast(U32)
+            nc.vector.tensor_copy(words, ctok[1][:].bitcast(U32).indirect(list2[:, entries(f)]))
+
+        def weave(f):
+            nc.scalar.copy(
+                cg[f].rearrange("p s t -> p (s t)").bitcast(F32).rearrange("p (s u) -> p s u", u=2),
+                cpair[f][:].rearrange("p u s d -> p (u s d)").bitcast(F32).rearrange("p (u s) -> p s u", u=2),
+            )
+
+        def w2_quantise(first, rounded, tag=None):
+            count = rounded[:].shape[1]
+            codes = sbuf([P, count * N], U32, "w2w%d" % first, tag=tag)
+            for j in range(count):
+                w2w[first + j] = codes[:, j * N : (j + 1) * N]
             nc.vector.quantize_mx(
-                out=cw[:].bitcast(FP8X4),
-                scales=cs[:, first * C : (first + count) * C],
-                in_=values.rearrange("p s t -> p (s t)"),
-            )
-            return cw
-
-        def layer2_product(f, v, codes, sums):
-            nc.tensor.matmul_mx(
-                out=sums,
-                lhsT=w2w[f][:, v * P : (v + 1) * P].bitcast(FP8X4),
-                lhsT_scale=w2s[:, f, v * P : (v + 1) * P],
-                rhs=codes.bitcast(FP8X4),
-                rhs_scale=cs[:, slots(f)],
-                start=True,
-                stop=True,
+                out=codes[:].bitcast(FP8X4),
+                scales=w2s[:, first : first + count, :].rearrange("p f n -> p (f n)"),
+                in_=rounded[:].rearrange("p f n t -> p (f n t)"),
             )
 
-        def layer2_products(pieces, codes, first, letter):
-            bank = psum.tile([P, len(pieces) * C], F32, name="y_bank", tag=letter)
-            for j, (f, v) in enumerate(pieces):
-                layer2_product(f, v, codes[:, slots(f - first)], bank[:, slots(j)])
-            return bank
+        def c_quantise(first, values, tag=None):
+            count = values.shape[1] // C
+            codes = sbuf([P, count * C], U32, "cw%d" % first, tag=tag)
+            nc.vector.quantize_mx(out=codes[:].bitcast(FP8X4), scales=cs[:, span(first, count)], in_=values.rearrange("p s t -> p (s t)"))
+            return codes
 
-        def layer2_copy(bank, letter):
-            sums = keep.tile([P, bank[:].shape[1]], F32, name="ysums" + letter, tag="w2raw3" if letter == "d" else "ysums" + letter, align_bytes=64)
-            nc.scalar.copy(sums[:], bank[:])
+        def layer2_products(first, count, v, codes, letter):
+            sums = psum.tile([P, count * C], F32, name="y_bank", tag=letter)
+            for j in range(count):
+                nc.tensor.matmul_mx(
+                    out=sums[:, slots(j)],
+                    lhsT=w2w[first + j][:, v * P : (v + 1) * P].bitcast(FP8X4),
+                    lhsT_scale=w2s[:, first + j, v * P : (v + 1) * P],
+                    rhs=codes[:, slots(j)].bitcast(FP8X4),
+                    rhs_scale=cs[:, slots(first + j)],
+                    start=True,
+                    stop=True,
+                )
             return sums
 
-        def layer2_sums(pieces, codes, first, letter):
-            return layer2_copy(layer2_products(pieces, codes, first, letter), letter)
+        def gate_for_scalar(first, count, v, sums):
+            gated = sbuf([P, count * C], F32, "gated%d%d" % (first, v))
+            nc.vector.tensor_tensor(gated[:], sums[:], g2[:, span(first, count)], MULT)
+            return gated
 
-        def layer2_scatter(v, sums, first, last):
-            nc.vector.tensor_tensor(
-                otok[v][:].indirect(list2[:, first * LIST_COLS : (last + 1) * LIST_COLS]),
-                sums,
-                g2[:, first * C : (last + 1) * C],
-                mybir.AluOpType.mult,
-            )
+        def scalar_scatter(first, count, v, gated):
+            nc.scalar.activation(out=otok[v][:].indirect(list2[:, list_span(first, count)]), in_=gated[:], func=COPY)
 
-        for f in range(E - 1):
-            layer2_gather_words(f)
+        def copy_for_vector(first, count, v, sums):
+            held = sbuf([P, count * C], F32, "ysums%d%d" % (first, v))
+            nc.scalar.copy(held[:], sums[:])
+            return held
+
+        def vector_scatter(first, count, v, held):
+            nc.vector.tensor_tensor(otok[v][:].indirect(list2[:, list_span(first, count)]), held[:], g2[:, span(first, count)], MULT)
+
         for d in range(2):
             for f in range(2):
-                layer2_gather_plane(f, d)
+                gather_plane(f, d)
         for d in range(2):
-            layer2_gather_plane(2, d)
-        for f in range(E - 1):
-            layer2_weave(f)
-        cw = c_quantise(0, cg[0], reuse.tile([P, C], U32, name="cw0", offset=6144, align_bytes=64))
-        first_sums = [layer2_sums([(0, v)], cw, 0, "ab"[v]) for v in range(2)]
-        w2_quantise(1, 2, reuse.tile([P, 2 * N], U32, name="w2w1", offset=1984, align_bytes=64))
-        cw = c_quantise(1, cgmid[:], keep.tile([P, 2 * C], U32, name="cw1", tag="cw1", align_bytes=64))
-        layer2_gather_words(3)
+            gather_plane(2, d)
+        for f in range(2):
+            gather_pair(f)
+            weave(f)
+        w2_quantise(0, w2b[0], tag="hlast")
+        codes = c_quantise(0, cg[0])
+        first_sums = [layer2_products(0, 1, v, codes, "ab"[v]) for v in range(2)]
         for d in range(2):
-            layer2_gather_plane(3, d)
-        layer2_weave(3)
-        banks = [layer2_products([(1, v), (2, v)], cw, 1, "cd"[v]) for v in range(2)]
-        middle_sums = [layer2_copy(banks[0], "c")]
-        w2b[3] = keep.tile([P, 1, N, 4], BF16, name="w2b3", tag="cw1", align_bytes=64)
-        scalar_round(w2b[3][:, 0], w2raw[3])
-        middle_sums.append(layer2_copy(banks[1], "d"))
+            gather_plane(3, d)
+        for f in (2, 3):
+            gather_pair(f)
+            weave(f)
         for v in range(2):
-            layer2_scatter(v, first_sums[v][:], 0, 0)
-        layer2_scatter(0, middle_sums[0][:], 1, 2)
-        cw = c_quantise(3, cg[3], keep.tile([P, C], U32, name="cw3", tag="ysumsa", align_bytes=64))
-        w2_quantise(3, 1, keep.tile([P, N], U32, name="w2w3", align_bytes=64))
-        layer2_scatter(1, middle_sums[1][:], 1, 2)
-        for v in range(2):
-            layer2_scatter(v, layer2_sums([(3, v)], cw, 3, "ef"[v])[:], 3, 3)
+            scalar_scatter(0, 1, v, gate_for_scalar(0, 1, v, first_sums[v]))
+        w2_quantise(1, w2b[1], tag="cpair1")
+        codes = c_quantise(1, cgmid[:])
+        middle_sums = [layer2_products(1, 2, v, codes, "cd"[v]) for v in range(2)]
+        w2b3 = sbuf([P, 1, N, 4], BF16, "w2b3", tag="gated00")
+        interleave(nc.vector.tensor_copy, w2b3[:, 0], w2raw[3])
+        held = copy_for_vector(1, 2, 0, middle_sums[0])
+        scalar_scatter(1, 2, 1, gate_for_scalar(1, 2, 1, middle_sums[1]))
+        w2_quantise(3, w2b3)
+        codes = c_quantise(3, cg[3])
+        last_sums = [layer2_products(3, 1, v, codes, "ef"[v]) for v in range(2)]
+        vector_scatter(1, 2, 0, held)
+        held = copy_for_vector(3, 1, 0, last_sums[0])
+        scalar_scatter(3, 1, 1, gate_for_scalar(3, 1, 1, last_sums[1]))
+        vector_scatter(3, 1, 0, held)
         for v in range(2):
             nc.sync.dma_start(out[v * P : (v + 1) * P, :], otok[v][:])

@@ -13,6 +13,7 @@ FP8X4 = mybir.dt.float8_e4m3fn_x4
 FP4X4 = mybir.dt.float4_e2m1fn_x4
 COPY = mybir.ActivationFunctionType.Copy
 MULT = mybir.AluOpType.mult
+ADD = mybir.AluOpType.add
 
 P = 128
 T = 512
@@ -29,6 +30,7 @@ def tile_moe_ser_none_kernel(tc, x_words, x_scales, w1_words, w1_scales, w2, gat
     nc = tc.nc
     with ExitStack() as ctx:
         keep = ctx.enter_context(tc.tile_pool(name="keep", bufs=1))
+        placed = ctx.enter_context(tc.tile_pool(name="placed", bufs=1))
         psum = ctx.enter_context(tc.psum_pool(name="psum", bufs=1))
 
         def slots(e):
@@ -74,24 +76,32 @@ def tile_moe_ser_none_kernel(tc, x_words, x_scales, w1_words, w1_scales, w2, gat
 
         g1 = gate_columns(g1rows, "g1")
 
-        w2raw = [keep.tile([P, 4, N], F32, name="w2raw%d" % f, tag="w2raw%d" % f, align_bytes=64)[:] for f in range(E)]
+        w2raw = [keep.tile([P, 4, N], F32, name="w2raw%d" % f, tag="w2raw%d" % f, align_bytes=64)[:] for f in range(E - 1)]
+        w2raw.append(placed.tile([P, 4, N], F32, name="w2raw3", offset=6144, align_bytes=64)[:])
         g2 = keep.tile([P, T], F32, name="g2", align_bytes=64)[:]
-        for f in (1, 0, 2, 3):
+        for f in range(E):
             nc.sync.dma_start(w2raw[f], w2[f].rearrange("(p j) n -> p j n", j=4))
         nc.sync.dma_start(g2, gate2)
 
+        def sbuf(shape, dtype, name, tag=None):
+            return keep.tile(shape, dtype, name=name, tag=tag or name, align_bytes=64)
+
+        def at(offset, shape, dtype, name):
+            return placed.tile(shape, dtype, name=name, offset=offset, align_bytes=64)
+
+        def span(first, count):
+            return slice(first * C, (first + count) * C)
+
+        def list_span(first, count):
+            return slice(first * LIST_COLS, (first + count) * LIST_COLS)
+
         xgw = []
-        xgs = keep.tile([P, T], U8, name="xgs", align_bytes=64)
-        hrow = [keep.tile([P, 2, P, 2], BF16, name="hrow%d" % e, tag="hrow%d" % e, align_bytes=64) for e in range(E)]
-        hzero = keep.tile([P, C], F32, name="hzero", align_bytes=64)
-        hfront = keep.tile([P, C // 2], F32, name="hfront", align_bytes=64)
-        hone = keep.tile([P, C], F32, name="hone", align_bytes=64)
-        hlast = keep.tile([P, 2 * C], F32, name="hlast", tag="hlast", align_bytes=64)
-        hlate = keep.tile([P, 3 * C], F32, name="hlate", tag="hlate", align_bytes=64)
-        ctok = [keep.tile([P, T], F32, name="ctok%d" % u, align_bytes=64) for u in range(2)]
+        xgs = sbuf([P, T], U8, "xgs")
+        hrow = [sbuf([P, 2, P, 2], BF16, "hrow%d" % e) for e in range(E - 1)] + [at(2048 - 512, [P, 2, P, 2], BF16, "hrow3")]
+        ctok = [sbuf([P, T], F32, "ctok%d" % u) for u in range(2)]
 
         def layer1_gather(e):
-            xgw.append(keep.tile([P, C], U32, name="xgw%d" % e, tag="xgw%d" % (e % 3), align_bytes=64))
+            xgw.append(sbuf([P, C], U32, "xgw%d" % e, tag="xgw%d" % (e % 3)))
             nc.vector.tensor_copy(xgw[e][:], xw[:].bitcast(U32).indirect(list1[:, entries(e)]))
             nc.vector.tensor_copy(xgs[:, slots(e)], xs[:].indirect(list1[:, entries(e)]))
 
@@ -112,27 +122,19 @@ def tile_moe_ser_none_kernel(tc, x_words, x_scales, w1_words, w1_scales, w2, gat
             nc.scalar.activation(out=rows, in_=sums, func=COPY, scale=g1[:, e : e + 1])
 
         def gate_on_vector(e, rows, sums):
-            nc.vector.tensor_scalar(out=rows, in0=sums, scalar1=g1[:, e : e + 1], scalar2=None, op0=mybir.AluOpType.mult)
+            nc.vector.tensor_scalar(out=rows, in0=sums, scalar1=g1[:, e : e + 1], scalar2=None, op0=MULT)
 
-        def layer1_turn(e, u, bank):
-            words = hrow[e][:].rearrange("s u p d -> s (u p d)").bitcast(F32)
-            nc.tensor.transpose(bank, words[:, u * P : (u + 1) * P], ident[:])
+        def turn(pieces, letter):
+            bank = psum.tile([P, len(pieces) * C], F32, name="turn_bank", tag=letter)
+            for j, (e, u) in enumerate(pieces):
+                words = hrow[e][:].rearrange("s u p d -> s (u p d)").bitcast(F32)
+                nc.tensor.transpose(bank[:, slots(j)], words[:, u * P : (u + 1) * P], ident[:])
+            return bank
 
-        def gpsimd_round(rounded, values):
-            nc.gpsimd.tensor_scalar(
-                out=rounded,
-                in0=values,
-                scalar1=1.0,
-                scalar2=0.0,
-                op0=mybir.AluOpType.mult,
-                op1=mybir.AluOpType.add,
-            )
-
-        def scalar_round(rounded, values):
-            nc.scalar.copy(
-                rounded.rearrange("p (c i) t -> p c t i", i=4),
-                values.rearrange("p t (c i) -> p c t i", i=4),
-            )
+        def turned(pieces, letter, copy):
+            held = sbuf([P, len(pieces) * C], F32, "turned%d%d" % pieces[0])
+            copy(held[:], turn(pieces, letter)[:])
+            return held
 
         layer1_gather(0)
         high = layer1_product(0, H // 2, H // 2, "b")
@@ -141,62 +143,44 @@ def tile_moe_ser_none_kernel(tc, x_words, x_scales, w1_words, w1_scales, w2, gat
         gate_on_scalar(0, *high)
         for quarter in quarters:
             gate_on_vector(0, *quarter)
-        first_banks = [psum.tile([P, C], F32, name="first_bank", tag=("f", "h")[u]) for u in range(2)]
-        for u in range(2):
-            layer1_turn(0, u, first_banks[u][:])
-        nc.vector.tensor_copy(hzero[:], first_banks[0][:])
-        nc.scalar.copy(hfront[:], first_banks[1][:, 0 : C // 2])
+        zero0 = turned([(0, 0)], "f", nc.vector.tensor_copy)
+        zero1_bank = turn([(0, 1)], "h")
+        front = sbuf([P, C // 2], F32, "front")
+        nc.scalar.copy(front[:], zero1_bank[:, 0 : C // 2])
         gate_on_scalar(1, *layer1_product(1, 0, H, "c"))
-        one_bank = psum.tile([P, C], F32, name="one_bank", tag="g")
-        late_bank = psum.tile([P, 3 * C], F32, name="late_bank", tag="e")
-        layer1_turn(1, 0, one_bank[:])
-        nc.scalar.copy(hone[:], one_bank[:])
-        hback = keep.tile([P, C // 2], F32, name="hback", tag="hrow1", align_bytes=64)
-        nc.scalar.copy(hback[:], first_banks[1][:, C // 2 : C])
-        last_bank = psum.tile([P, 2 * C], F32, name="last_bank", tag="d")
+        one0 = turned([(1, 0)], "g", nc.scalar.copy)
+        back = sbuf([P, C // 2], F32, "back", tag="hrow1")
+        nc.scalar.copy(back[:], zero1_bank[:, C // 2 : C])
         for e in range(2, E):
             layer1_gather(e)
             gate_on_scalar(e, *layer1_product(e, 0, H, ("b", "a")[e - 2]))
-            layer1_turn(e, 0, last_bank[:, slots(e - 2)])
-        nc.scalar.copy(hlast[:], last_bank[:])
-        for e in range(1, E):
-            layer1_turn(e, 1, late_bank[:, slots(e - 1)])
-        nc.scalar.copy(hlate[:], late_bank[:])
+        last0 = turned([(2, 0), (3, 0)], "d", nc.scalar.copy)
+        late1 = turned([(1, 1), (2, 1), (3, 1)], "e", nc.scalar.copy)
         half = LIST_COLS // 2
         for u, first, last, words in (
-            (0, 0, LIST_COLS, hzero),
-            (1, 0, half, hfront),
-            (0, LIST_COLS, 2 * LIST_COLS, hone),
-            (1, half, LIST_COLS, hback),
-            (0, 2 * LIST_COLS, 4 * LIST_COLS, hlast),
-            (1, LIST_COLS, 4 * LIST_COLS, hlate),
+            (0, 0, LIST_COLS, zero0),
+            (1, 0, half, front),
+            (0, LIST_COLS, 2 * LIST_COLS, one0),
+            (1, half, LIST_COLS, back),
+            (0, 2 * LIST_COLS, 4 * LIST_COLS, last0),
+            (1, LIST_COLS, 4 * LIST_COLS, late1),
         ):
             nc.vector.tensor_copy(ctok[u][:].indirect(list1[:, first:last]), words[:])
-        w2b = {
-            0: keep.tile([P, 1, N, 4], BF16, name="w2b0", tag="hrow3", align_bytes=64),
-            1: keep.tile([P, 2, N, 4], BF16, name="w2b1", align_bytes=64),
-        }
-        scalar_round(w2b[0][:, 0], w2raw[0])
-        for f in (1, 2):
-            gpsimd_round(w2b[1][:, f - 1], w2raw[f].rearrange("p t n -> p n t"))
-        cplane = [keep.tile([P, T], BF16, name="cplane%d" % d, tag=("cplane0", "w2raw2")[d], align_bytes=64) for d in range(2)]
+
+        def gpsimd_round(rounded, values):
+            nc.gpsimd.tensor_scalar(out=rounded, in0=values, scalar1=1.0, scalar2=0.0, op0=MULT, op1=ADD)
+
+        w2b = [sbuf([P, N, 4], BF16, "w2b0"), at(0, [P, N, 4], BF16, "w2b1"), sbuf([P, N, 4], BF16, "w2b2"), at(2048, [P, N, 4], BF16, "w2b3")]
+        for f in (1, 3):
+            nc.scalar.copy(w2b[f][:].rearrange("p (c i) t -> p c t i", i=4), w2raw[f].rearrange("p t (c i) -> p c t i", i=4))
+        for f in (0, 2):
+            gpsimd_round(w2b[f][:], w2raw[f].rearrange("p t n -> p n t"))
+        cplane = [sbuf([P, T], BF16, "cplane%d" % d, tag=("cplane0", "w2raw2")[d]) for d in range(2)]
         pairs = ctok[0][:].bitcast(BF16).rearrange("p (s d) -> p s d", d=2)
-        nc.scalar.copy(cplane[0][:], pairs[:, :, 0])
-        gpsimd_round(cplane[1][:], pairs[:, :, 1])
+        for d in range(2):
+            gpsimd_round(cplane[d][:], pairs[:, :, d])
 
-        def sbuf(shape, dtype, name, tag=None):
-            return keep.tile(shape, dtype, name=name, tag=tag or name, align_bytes=64)
-
-        def span(first, count):
-            return slice(first * C, (first + count) * C)
-
-        def list_span(first, count):
-            return slice(first * LIST_COLS, (first + count) * LIST_COLS)
-
-        def interleave(copy, rounded, values):
-            copy(rounded.rearrange("p (c i) t -> p c t i", i=4), values.rearrange("p t (c i) -> p c t i", i=4))
-
-        cpair = [sbuf([P, 2, C, 2], BF16, "cpair%d" % f) for f in range(E)]
+        cpair = [at((6208, 9216, 7232, 5184)[f], [P, 2, C, 2], BF16, "cpair%d" % f) for f in range(E)]
         cgmid = sbuf([P, 2 * C, 4], BF16, "cgmid")
         cg = [sbuf([P, C, 4], BF16, "cg0")[:], cgmid[:, slots(0), :], cgmid[:, slots(1), :], sbuf([P, C, 4], BF16, "cg3")[:]]
         w2s = sbuf([P, E, N], U8, "w2s")
@@ -204,10 +188,10 @@ def tile_moe_ser_none_kernel(tc, x_words, x_scales, w1_words, w1_scales, w2, gat
         otok = [sbuf([P, T], F32, "otok%d" % v) for v in range(2)]
         w2w = {}
 
-        def gather_plane(f, d):
+        def gather_values(f, d):
             nc.scalar.activation(out=cpair[f][:, 0, :, d], in_=cplane[d][:].indirect(list2[:, entries(f)]), func=COPY)
 
-        def gather_pair(f):
+        def gather_pairs(f):
             words = cpair[f][:, 1].rearrange("p s d -> p (s d)").bitcast(U32)
             nc.vector.tensor_copy(words, ctok[1][:].bitcast(U32).indirect(list2[:, entries(f)]))
 
@@ -217,20 +201,13 @@ def tile_moe_ser_none_kernel(tc, x_words, x_scales, w1_words, w1_scales, w2, gat
                 cpair[f][:].rearrange("p u s d -> p (u s d)").bitcast(F32).rearrange("p (u s) -> p s u", u=2),
             )
 
-        def w2_quantise(first, rounded, tag=None):
-            count = rounded[:].shape[1]
-            codes = sbuf([P, count * N], U32, "w2w%d" % first, tag=tag)
-            for j in range(count):
-                w2w[first + j] = codes[:, j * N : (j + 1) * N]
-            nc.vector.quantize_mx(
-                out=codes[:].bitcast(FP8X4),
-                scales=w2s[:, first : first + count, :].rearrange("p f n -> p (f n)"),
-                in_=rounded[:].rearrange("p f n t -> p (f n t)"),
-            )
+        def w2_quantise(f, codes):
+            w2w[f] = codes
+            nc.vector.quantize_mx(out=w2w[f][:].bitcast(FP8X4), scales=w2s[:, f, :], in_=w2b[f][:].rearrange("p n t -> p (n t)"))
 
-        def c_quantise(first, values, tag=None):
+        def c_quantise(first, values):
             count = values.shape[1] // C
-            codes = sbuf([P, count * C], U32, "cw%d" % first, tag=tag)
+            codes = sbuf([P, count * C], U32, "cw%d" % first)
             nc.vector.quantize_mx(out=codes[:].bitcast(FP8X4), scales=cs[:, span(first, count)], in_=values.rearrange("p s t -> p (s t)"))
             return codes
 
@@ -248,53 +225,45 @@ def tile_moe_ser_none_kernel(tc, x_words, x_scales, w1_words, w1_scales, w2, gat
                 )
             return sums
 
-        def gate_for_scalar(first, count, v, sums):
+        def gate_sums(first, count, v, sums):
             gated = sbuf([P, count * C], F32, "gated%d%d" % (first, v))
             nc.vector.tensor_tensor(gated[:], sums[:], g2[:, span(first, count)], MULT)
             return gated
 
+        def window(first, count, v):
+            return otok[v][:].indirect(list2[:, list_span(first, count)])
+
         def scalar_scatter(first, count, v, gated):
-            nc.scalar.activation(out=otok[v][:].indirect(list2[:, list_span(first, count)]), in_=gated[:], func=COPY)
+            nc.scalar.activation(out=window(first, count, v), in_=gated[:], func=COPY)
 
-        def copy_for_vector(first, count, v, sums):
-            held = sbuf([P, count * C], F32, "ysums%d%d" % (first, v))
-            nc.scalar.copy(held[:], sums[:])
-            return held
-
-        def vector_scatter(first, count, v, held):
-            nc.vector.tensor_tensor(otok[v][:].indirect(list2[:, list_span(first, count)]), held[:], g2[:, span(first, count)], MULT)
-
+        w2_quantise(0, sbuf([P, N], U32, "w2w0", tag="w2raw1"))
         for d in range(2):
-            for f in range(2):
-                gather_plane(f, d)
-        for d in range(2):
-            gather_plane(2, d)
-        for f in range(2):
-            gather_pair(f)
+            for f in range(E - 1):
+                gather_values(f, d)
+        for f in range(E):
+            gather_pairs(f)
+        for f in range(E - 1):
             weave(f)
-        w2_quantise(0, w2b[0], tag="hlast")
+        for d in range(2):
+            gather_values(3, d)
+        weave(3)
         codes = c_quantise(0, cg[0])
         first_sums = [layer2_products(0, 1, v, codes, "ab"[v]) for v in range(2)]
-        for d in range(2):
-            gather_plane(3, d)
-        for f in (2, 3):
-            gather_pair(f)
-            weave(f)
-        for v in range(2):
-            scalar_scatter(0, 1, v, gate_for_scalar(0, 1, v, first_sums[v]))
-        w2_quantise(1, w2b[1], tag="cpair1")
+        for f in (1, 2):
+            w2_quantise(f, at((8192 + 64, 10240 - 64)[f - 1], [P, N], U32, "w2w%d" % f))
         codes = c_quantise(1, cgmid[:])
         middle_sums = [layer2_products(1, 2, v, codes, "cd"[v]) for v in range(2)]
-        w2b3 = sbuf([P, 1, N, 4], BF16, "w2b3", tag="gated00")
-        interleave(nc.vector.tensor_copy, w2b3[:, 0], w2raw[3])
-        held = copy_for_vector(1, 2, 0, middle_sums[0])
-        scalar_scatter(1, 2, 1, gate_for_scalar(1, 2, 1, middle_sums[1]))
-        w2_quantise(3, w2b3)
+        for v in range(2):
+            scalar_scatter(0, 1, v, gate_sums(0, 1, v, first_sums[v]))
+        w2_quantise(3, at(4096 + 128, [P, N], U32, "w2w3"))
         codes = c_quantise(3, cg[3])
         last_sums = [layer2_products(3, 1, v, codes, "ef"[v]) for v in range(2)]
-        vector_scatter(1, 2, 0, held)
-        held = copy_for_vector(3, 1, 0, last_sums[0])
-        scalar_scatter(3, 1, 1, gate_for_scalar(3, 1, 1, last_sums[1]))
-        vector_scatter(3, 1, 0, held)
+        middle_gated = [gate_sums(1, 2, v, middle_sums[v]) for v in range(2)]
+        nc.vector.tensor_copy(window(1, 2, 0), middle_gated[0][:])
+        last_held = sbuf([P, C], F32, "last_held")
+        nc.scalar.copy(last_held[:], last_sums[0][:])
+        scalar_scatter(1, 2, 1, middle_gated[1])
+        scalar_scatter(3, 1, 1, gate_sums(3, 1, 1, last_sums[1]))
+        nc.vector.tensor_tensor(window(3, 1, 0), last_held[:], g2[:, slots(3)], MULT)
         for v in range(2):
             nc.sync.dma_start(out[v * P : (v + 1) * P, :], otok[v][:])

@@ -76,8 +76,8 @@ def tile_moe_ser_none_kernel(tc, x_words, x_scales, w1_words, w1_scales, w2, gat
 
         g1 = gate_columns(g1rows, "g1")
 
-        w2raw = [keep.tile([P, 4, N], F32, name="w2raw%d" % f, tag="w2raw%d" % f, align_bytes=64)[:] for f in range(E - 1)]
-        w2raw.append(placed.tile([P, 4, N], F32, name="w2raw3", offset=6144, align_bytes=64)[:])
+        w2raw = [keep.tile([P, 4, N], F32, name="w2raw%d" % f, tag="w2raw%d" % f, align_bytes=64)[:] for f in (0, 1, 3)]
+        w2raw[2:2] = [placed.tile([P, 4, N], F32, name="w2raw2", offset=6144, align_bytes=64)[:]]
         g2 = keep.tile([P, T], F32, name="g2", align_bytes=64)[:]
         for f in range(E):
             nc.sync.dma_start(w2raw[f], w2[f].rearrange("(p j) n -> p j n", j=4))
@@ -170,18 +170,20 @@ def tile_moe_ser_none_kernel(tc, x_words, x_scales, w1_words, w1_scales, w2, gat
         def gpsimd_round(rounded, values):
             nc.gpsimd.tensor_scalar(out=rounded, in0=values, scalar1=1.0, scalar2=0.0, op0=MULT, op1=ADD)
 
-        w2b = [sbuf([P, N, 4], BF16, "w2b0"), at(0, [P, N, 4], BF16, "w2b1"), sbuf([P, N, 4], BF16, "w2b2"), at(2048, [P, N, 4], BF16, "w2b3")]
-        for f in (1, 3):
+        def scalar_round(f):
             nc.scalar.copy(w2b[f][:].rearrange("p (c i) t -> p c t i", i=4), w2raw[f].rearrange("p t (c i) -> p c t i", i=4))
-        for f in (0, 2):
-            gpsimd_round(w2b[f][:], w2raw[f].rearrange("p t n -> p n t"))
-        cplane = [sbuf([P, T], BF16, "cplane%d" % d, tag=("cplane0", "w2raw2")[d]) for d in range(2)]
+
+        w2b = [sbuf([P, N, 4], BF16, "w2b0"), at(0, [P, N, 4], BF16, "w2b1"), at(2048, [P, N, 4], BF16, "w2b2")]
+        gpsimd_round(w2b[0][:], w2raw[0].rearrange("p t n -> p n t"))
+        for f in (1, 2):
+            scalar_round(f)
+        cplane = [sbuf([P, T], BF16, "cplane%d" % d) for d in range(2)]
         pairs = ctok[0][:].bitcast(BF16).rearrange("p (s d) -> p s d", d=2)
         for d in range(2):
-            gpsimd_round(cplane[d][:], pairs[:, :, d])
+            nc.scalar.copy(cplane[d][:], pairs[:, :, d])
 
-        cpair = [at((6208, 9216, 7232, 5184)[f], [P, 2, C, 2], BF16, "cpair%d" % f) for f in range(E)]
-        cgmid = sbuf([P, 2 * C, 4], BF16, "cgmid")
+        cpair = [at((6208, 9216, 7232)[f], [P, 2, C, 2], BF16, "cpair%d" % f) for f in range(E - 1)]
+        cgmid = sbuf([P, 2 * C, 4], BF16, "cgmid", tag="cplane1")
         cg = [sbuf([P, C, 4], BF16, "cg0")[:], cgmid[:, slots(0), :], cgmid[:, slots(1), :], sbuf([P, C, 4], BF16, "cg3")[:]]
         w2s = sbuf([P, E, N], U8, "w2s")
         cs = sbuf([P, T], U8, "cs")
@@ -191,9 +193,9 @@ def tile_moe_ser_none_kernel(tc, x_words, x_scales, w1_words, w1_scales, w2, gat
         def gather_values(f, d):
             nc.scalar.activation(out=cpair[f][:, 0, :, d], in_=cplane[d][:].indirect(list2[:, entries(f)]), func=COPY)
 
-        def gather_pairs(f):
-            words = cpair[f][:, 1].rearrange("p s d -> p (s d)").bitcast(U32)
-            nc.vector.tensor_copy(words, ctok[1][:].bitcast(U32).indirect(list2[:, entries(f)]))
+        def gather_pairs(f, u):
+            words = cpair[f][:, u].rearrange("p s d -> p (s d)").bitcast(U32)
+            nc.vector.tensor_copy(words, ctok[u][:].bitcast(U32).indirect(list2[:, entries(f)]))
 
         def weave(f):
             nc.scalar.copy(
@@ -238,32 +240,34 @@ def tile_moe_ser_none_kernel(tc, x_words, x_scales, w1_words, w1_scales, w2, gat
 
         w2_quantise(0, sbuf([P, N], U32, "w2w0", tag="w2raw1"))
         for d in range(2):
-            for f in range(E - 1):
+            for f in range(2):
                 gather_values(f, d)
-        for f in range(E):
-            gather_pairs(f)
+        for f, u in ((0, 1), (1, 1), (2, 0), (2, 1)):
+            gather_pairs(f, u)
         for f in range(E - 1):
             weave(f)
-        for d in range(2):
-            gather_values(3, d)
-        weave(3)
+        w2b.append(at(4224, [P, N, 4], BF16, "w2b3"))
+        scalar_round(3)
         codes = c_quantise(0, cg[0])
         first_sums = [layer2_products(0, 1, v, codes, "ab"[v]) for v in range(2)]
         for f in (1, 2):
             w2_quantise(f, at((8192 + 64, 10240 - 64)[f - 1], [P, N], U32, "w2w%d" % f))
         codes = c_quantise(1, cgmid[:])
         middle_sums = [layer2_products(1, 2, v, codes, "cd"[v]) for v in range(2)]
-        for v in range(2):
-            scalar_scatter(0, 1, v, gate_sums(0, 1, v, first_sums[v]))
-        w2_quantise(3, at(4096 + 128, [P, N], U32, "w2w3"))
+        scalar_scatter(0, 1, 0, gate_sums(0, 1, 0, first_sums[0]))
+        cpair.append(at(7232, [P, 2, C, 2], BF16, "cpair3"))
+        for u in range(2):
+            gather_pairs(3, u)
+        weave(3)
+        scalar_scatter(0, 1, 1, gate_sums(0, 1, 1, first_sums[1]))
+        middle_gated = [gate_sums(1, 2, v, middle_sums[v]) for v in range(2)]
+        w2_quantise(3, sbuf([P, N], U32, "w2w3", tag="gated00"))
         codes = c_quantise(3, cg[3])
         last_sums = [layer2_products(3, 1, v, codes, "ef"[v]) for v in range(2)]
-        middle_gated = [gate_sums(1, 2, v, middle_sums[v]) for v in range(2)]
         nc.vector.tensor_copy(window(1, 2, 0), middle_gated[0][:])
-        last_held = sbuf([P, C], F32, "last_held")
-        nc.scalar.copy(last_held[:], last_sums[0][:])
         scalar_scatter(1, 2, 1, middle_gated[1])
-        scalar_scatter(3, 1, 1, gate_sums(3, 1, 1, last_sums[1]))
-        nc.vector.tensor_tensor(window(3, 1, 0), last_held[:], g2[:, slots(3)], MULT)
+        last_gated = [gate_sums(3, 1, v, last_sums[v]) for v in range(2)]
+        scalar_scatter(3, 1, 1, last_gated[1])
+        nc.vector.tensor_copy(window(3, 1, 0), last_gated[0][:])
         for v in range(2):
             nc.sync.dma_start(out[v * P : (v + 1) * P, :], otok[v][:])

@@ -76,8 +76,8 @@ def tile_moe_ser_none_kernel(tc, x_words, x_scales, w1_words, w1_scales, w2, gat
 
         g1 = gate_columns(g1rows, "g1")
 
-        w2raw = [keep.tile([P, 4, N], F32, name="w2raw%d" % f, tag="w2raw%d" % f, align_bytes=64)[:] for f in (0, 1, 3)]
-        w2raw[2:2] = [placed.tile([P, 4, N], F32, name="w2raw2", offset=6144, align_bytes=64)[:]]
+        w2raw = [keep.tile([P, 4, N], F32, name="w2raw%d" % f, tag="w2raw%d" % f, align_bytes=64)[:] for f in range(E - 1)]
+        w2raw.append(placed.tile([P, 4, N], F32, name="w2raw3", offset=6144, align_bytes=64)[:])
         g2 = keep.tile([P, T], F32, name="g2", align_bytes=64)[:]
         for f in range(E):
             nc.sync.dma_start(w2raw[f], w2[f].rearrange("(p j) n -> p j n", j=4))
@@ -173,9 +173,10 @@ def tile_moe_ser_none_kernel(tc, x_words, x_scales, w1_words, w1_scales, w2, gat
         def scalar_round(f):
             nc.scalar.copy(w2b[f][:].rearrange("p (c i) t -> p c t i", i=4), w2raw[f].rearrange("p t (c i) -> p c t i", i=4))
 
-        w2b = [sbuf([P, N, 4], BF16, "w2b0"), at(0, [P, N, 4], BF16, "w2b1"), at(2048, [P, N, 4], BF16, "w2b2")]
-        gpsimd_round(w2b[0][:], w2raw[0].rearrange("p t n -> p n t"))
-        for f in (1, 2):
+        w2b = [sbuf([P, N, 4], BF16, "w2b0"), at(0, [P, N, 4], BF16, "w2b1"), sbuf([P, N, 4], BF16, "w2b2"), at(2048, [P, N, 4], BF16, "w2b3")]
+        for f in (0, 2):
+            gpsimd_round(w2b[f][:], w2raw[f].rearrange("p t n -> p n t"))
+        for f in (1, 3):
             scalar_round(f)
         cplane = [sbuf([P, T], BF16, "cplane%d" % d) for d in range(2)]
         pairs = ctok[0][:].bitcast(BF16).rearrange("p (s d) -> p s d", d=2)
@@ -246,8 +247,6 @@ def tile_moe_ser_none_kernel(tc, x_words, x_scales, w1_words, w1_scales, w2, gat
             gather_pairs(f, u)
         for f in range(E - 1):
             weave(f)
-        w2b.append(at(4224, [P, N, 4], BF16, "w2b3"))
-        scalar_round(3)
         codes = c_quantise(0, cg[0])
         first_sums = [layer2_products(0, 1, v, codes, "ab"[v]) for v in range(2)]
         for f in (1, 2):

@@ -170,21 +170,21 @@ def tile_moe_ser_none_kernel(tc, x_words, x_scales, w1_words, w1_scales, w2, gat
         def gpsimd_round(rounded, values):
             nc.gpsimd.tensor_scalar(out=rounded, in0=values, scalar1=1.0, scalar2=0.0, op0=MULT, op1=ADD)
 
-        def scalar_round(f):
-            nc.scalar.copy(w2b[f][:].rearrange("p (c i) t -> p c t i", i=4), w2raw[f].rearrange("p t (c i) -> p c t i", i=4))
+        def scalar_round(rounded, values):
+            nc.scalar.copy(rounded.rearrange("p (c i) t -> p c t i", i=4), values.rearrange("p t (c i) -> p c t i", i=4))
 
         w2b = [sbuf([P, N, 4], BF16, "w2b0"), at(0, [P, N, 4], BF16, "w2b1"), sbuf([P, N, 4], BF16, "w2b2"), at(2048, [P, N, 4], BF16, "w2b3")]
-        for f in (0, 2):
-            gpsimd_round(w2b[f][:], w2raw[f].rearrange("p t n -> p n t"))
-        for f in (1, 3):
-            scalar_round(f)
+        for f, first, last in ((0, 0, N), (2, 0, N), (3, N // 2, N)):
+            gpsimd_round(w2b[f][:, first:last], w2raw[f][:, :, first:last].rearrange("p t n -> p n t"))
+        for f, first, last in ((1, 0, N), (3, 0, N // 2)):
+            scalar_round(w2b[f][:, first:last], w2raw[f][:, :, first:last])
         cplane = [sbuf([P, T], BF16, "cplane%d" % d) for d in range(2)]
         pairs = ctok[0][:].bitcast(BF16).rearrange("p (s d) -> p s d", d=2)
         for d in range(2):
             nc.scalar.copy(cplane[d][:], pairs[:, :, d])
 
-        cpair = [at((6208, 9216, 7232)[f], [P, 2, C, 2], BF16, "cpair%d" % f) for f in range(E - 1)]
-        cgmid = sbuf([P, 2 * C, 4], BF16, "cgmid", tag="cplane1")
+        cpair = [at((6208, 9216, 7232, 5184)[f], [P, 2, C, 2], BF16, "cpair%d" % f) for f in range(E)]
+        cgmid = sbuf([P, 2 * C, 4], BF16, "cgmid", tag="cplane0")
         cg = [sbuf([P, C, 4], BF16, "cg0")[:], cgmid[:, slots(0), :], cgmid[:, slots(1), :], sbuf([P, C, 4], BF16, "cg3")[:]]
         w2s = sbuf([P, E, N], U8, "w2s")
         cs = sbuf([P, T], U8, "cs")
@@ -243,30 +243,31 @@ def tile_moe_ser_none_kernel(tc, x_words, x_scales, w1_words, w1_scales, w2, gat
         for d in range(2):
             for f in range(2):
                 gather_values(f, d)
+        gather_values(3, 0)
         for f, u in ((0, 1), (1, 1), (2, 0), (2, 1)):
             gather_pairs(f, u)
         for f in range(E - 1):
             weave(f)
+        gather_values(3, 1)
         codes = c_quantise(0, cg[0])
         first_sums = [layer2_products(0, 1, v, codes, "ab"[v]) for v in range(2)]
+        gather_pairs(3, 1)
+        weave(3)
         for f in (1, 2):
             w2_quantise(f, at((8192 + 64, 10240 - 64)[f - 1], [P, N], U32, "w2w%d" % f))
         codes = c_quantise(1, cgmid[:])
         middle_sums = [layer2_products(1, 2, v, codes, "cd"[v]) for v in range(2)]
-        scalar_scatter(0, 1, 0, gate_sums(0, 1, 0, first_sums[0]))
-        cpair.append(at(7232, [P, 2, C, 2], BF16, "cpair3"))
-        for u in range(2):
-            gather_pairs(3, u)
-        weave(3)
-        scalar_scatter(0, 1, 1, gate_sums(0, 1, 1, first_sums[1]))
-        middle_gated = [gate_sums(1, 2, v, middle_sums[v]) for v in range(2)]
-        w2_quantise(3, sbuf([P, N], U32, "w2w3", tag="gated00"))
+        for v in range(2):
+            scalar_scatter(0, 1, v, gate_sums(0, 1, v, first_sums[v]))
+        w2_quantise(3, at(4096 + 128, [P, N], U32, "w2w3"))
         codes = c_quantise(3, cg[3])
         last_sums = [layer2_products(3, 1, v, codes, "ef"[v]) for v in range(2)]
+        middle_gated = [gate_sums(1, 2, v, middle_sums[v]) for v in range(2)]
         nc.vector.tensor_copy(window(1, 2, 0), middle_gated[0][:])
+        last_held = sbuf([P, C], F32, "last_held")
+        nc.scalar.copy(last_held[:], last_sums[0][:])
         scalar_scatter(1, 2, 1, middle_gated[1])
-        last_gated = [gate_sums(3, 1, v, last_sums[v]) for v in range(2)]
-        scalar_scatter(3, 1, 1, last_gated[1])
-        nc.vector.tensor_copy(window(3, 1, 0), last_gated[0][:])
+        scalar_scatter(3, 1, 1, gate_sums(3, 1, 1, last_sums[1]))
+        nc.vector.tensor_tensor(window(3, 1, 0), last_held[:], g2[:, slots(3)], MULT)
         for v in range(2):
             nc.sync.dma_start(out[v * P : (v + 1) * P, :], otok[v][:])

@@ -151,10 +151,14 @@ def tile_moe_ser_none_kernel(tc, x_words, x_scales, w1_words, w1_scales, w2, gat
         one0 = turned([(1, 0)], "g", nc.scalar.copy)
         back = sbuf([P, C // 2], F32, "back", tag="hrow1")
         nc.scalar.copy(back[:], zero1_bank[:, C // 2 : C])
+        late_sums = {}
         for e in range(2, E):
             layer1_gather(e)
-            gate_on_scalar(e, *layer1_product(e, 0, H, ("b", "a")[e - 2]))
+            late_sums[e] = layer1_product(e, 0, H, ("b", "a")[e - 2])
+            gate_on_scalar(e, late_sums[e][0][:, 0], late_sums[e][1][:, 0])
         last0 = turned([(2, 0), (3, 0)], "d", nc.scalar.copy)
+        for e in range(2, E):
+            gate_on_scalar(e, late_sums[e][0][:, 1], late_sums[e][1][:, 1])
         late1 = turned([(1, 1), (2, 1), (3, 1)], "e", nc.scalar.copy)
         half = LIST_COLS // 2
         for u, first, last, words in (

@@ -144,13 +144,9 @@ def tile_moe_ser_none_kernel(tc, x_words, x_scales, w1_words, w1_scales, w2, gat
         for quarter in quarters:
             gate_on_vector(0, *quarter)
         zero0 = turned([(0, 0)], "f", nc.vector.tensor_copy)
-        zero1_bank = turn([(0, 1)], "h")
-        front = sbuf([P, C // 2], F32, "front")
-        nc.scalar.copy(front[:], zero1_bank[:, 0 : C // 2])
+        zero1 = turned([(0, 1)], "h", nc.scalar.copy)
         gate_on_scalar(1, *layer1_product(1, 0, H, "c"))
         one0 = turned([(1, 0)], "g", nc.scalar.copy)
-        back = sbuf([P, C // 2], F32, "back", tag="hrow1")
-        nc.scalar.copy(back[:], zero1_bank[:, C // 2 : C])
         late_sums = {}
         for e in range(2, E):
             layer1_gather(e)
@@ -162,14 +158,14 @@ def tile_moe_ser_none_kernel(tc, x_words, x_scales, w1_words, w1_scales, w2, gat
         late1 = turned([(1, 1), (2, 1), (3, 1)], "e", nc.scalar.copy)
         half = LIST_COLS // 2
         for u, first, last, words in (
-            (0, 0, LIST_COLS, zero0),
-            (1, 0, half, front),
-            (0, LIST_COLS, 2 * LIST_COLS, one0),
-            (1, half, LIST_COLS, back),
-            (0, 2 * LIST_COLS, 4 * LIST_COLS, last0),
-            (1, LIST_COLS, 4 * LIST_COLS, late1),
+            (0, 0, LIST_COLS, zero0[:]),
+            (1, 0, half, zero1[:, 0 : C // 2]),
+            (0, LIST_COLS, 2 * LIST_COLS, one0[:]),
+            (1, half, LIST_COLS, zero1[:, C // 2 : C]),
+            (0, 2 * LIST_COLS, 4 * LIST_COLS, last0[:]),
+            (1, LIST_COLS, 4 * LIST_COLS, late1[:]),
         ):
-            nc.vector.tensor_copy(ctok[u][:].indirect(list1[:, first:last]), words[:])
+            nc.vector.tensor_copy(ctok[u][:].indirect(list1[:, first:last]), words)
 
         def gpsimd_round(rounded, values):
             nc.gpsimd.tensor_scalar(out=rounded, in0=values, scalar1=1.0, scalar2=0.0, op0=MULT, op1=ADD)

from contextlib import ExitStack

import concourse.mybir as mybir
from concourse.masks import make_identity

F32 = mybir.dt.float32
BF16 = mybir.dt.bfloat16
I32 = mybir.dt.int32
U32 = mybir.dt.uint32
U16 = mybir.dt.uint16
U8 = mybir.dt.uint8
FP8X4 = mybir.dt.float8_e4m3fn_x4
FP4X4 = mybir.dt.float4_e2m1fn_x4
COPY = mybir.ActivationFunctionType.Copy
MULT = mybir.AluOpType.mult
ADD = mybir.AluOpType.add

P = 128
T = 512
H = 512
N = 256
E = 4
C = 128
LIST_COLS = C // 16

FLOPS = 2 * T * 512 * H + 2 * T * H * N


def tile_moe_ser_none_kernel(tc, x_words, x_scales, w1_words, w1_scales, w2, gate1, gate2, offs, offs2, out):
    nc = tc.nc
    with ExitStack() as ctx:
        keep = ctx.enter_context(tc.tile_pool(name="keep", bufs=1))
        placed = ctx.enter_context(tc.tile_pool(name="placed", bufs=1))
        psum = ctx.enter_context(tc.psum_pool(name="psum", bufs=1))

        def slots(e):
            return slice(e * C, (e + 1) * C)

        def entries(e):
            return slice(e * LIST_COLS, (e + 1) * LIST_COLS)

        list1 = keep.tile([P, T // 16], U16, name="list1")
        list2 = keep.tile([P, T // 16], U16, name="list2")
        xw = keep.tile([P, T], I32, name="xw", align_bytes=64)
        xs = keep.tile([P, T], U8, name="xs", align_bytes=64)
        w1pair = [keep.tile([P, 2, 2 * H], U8, name="w1pair%d" % j, align_bytes=64) for j in range(2)]
        w1s = keep.tile([P, E, H], U8, name="w1s", align_bytes=64)
        g1rows = keep.tile([P, C], F32, name="g1rows", align_bytes=64)
        ident = keep.tile([P, P], F32, name="ident")

        nc.gpsimd.memset(xs[:].bitcast(I32), 0)
        nc.gpsimd.memset(g1rows[:], 0.0)
        nc.vector.memset(w1s[:].rearrange("p e n -> p (e n)").bitcast(I32), 0)

        xs_rows = x_scales[0].rearrange("(q r) n -> r q n", r=4)
        w1s_rows = w1_scales[:, 0].rearrange("e (q r) n -> r q e n", r=4)
        make_identity(nc, ident[:])
        nc.sync.dma_start(list1[:], offs)
        nc.sync.dma_start(xw[:], x_words[0].rearrange("p t d -> p (t d)").bitcast(I32))
        for r in range(4):
            nc.sync.dma_start(xs[r:P:32, :].bitcast(I32), xs_rows[r].bitcast(I32))
        nc.sync.dma_start(g1rows[0:E, :], gate1[0].rearrange("(e c) -> e c", c=C))
        nc.sync.dma_start(w1pair[0][:].bitcast(I32), w1_words[0:2, 0].rearrange("e p n -> p e n").bitcast(I32))
        for r in range(4):
            nc.sync.dma_start(w1s[r:P:32, :, :].bitcast(I32), w1s_rows[r].bitcast(I32))
        nc.sync.dma_start(w1pair[1][:].bitcast(I32), w1_words[2:4, 0].rearrange("e p n -> p e n").bitcast(I32))
        w1w = [w1pair[e // 2][:, e % 2, :] for e in range(E)]
        nc.sync.dma_start(list2[:], offs2)

        def gate_columns(rows, name):
            bank = psum.tile([P, 512], F32, name="gate_bank", tag="a")
            nc.tensor.transpose(bank[:, 0:P], rows[:], ident[:])
            cols = keep.tile([P, E], F32, name=name)
            nc.scalar.copy(cols[:], bank[:, 0:E])
            return cols

        g1 = gate_columns(g1rows, "g1")

        w2raw = [keep.tile([P, 4, N], F32, name="w2raw%d" % f, tag="w2raw%d" % f, align_bytes=64)[:] for f in range(E - 1)]
        w2raw.append(placed.tile([P, 4, N], F32, name="w2raw3", offset=6144, align_bytes=64)[:])
        g2 = keep.tile([P, T], F32, name="g2", align_bytes=64)[:]
        for f in range(E):
            nc.sync.dma_start(w2raw[f], w2[f].rearrange("(p j) n -> p j n", j=4))
        nc.sync.dma_start(g2, gate2)

        def sbuf(shape, dtype, name, tag=None):
            return keep.tile(shape, dtype, name=name, tag=tag or name, align_bytes=64)

        def at(offset, shape, dtype, name):
            return placed.tile(shape, dtype, name=name, offset=offset, align_bytes=64)

        def span(first, count):
            return slice(first * C, (first + count) * C)

        def list_span(first, count):
            return slice(first * LIST_COLS, (first + count) * LIST_COLS)

        xgw = []
        xgs = sbuf([P, T], U8, "xgs")
        hrow = [sbuf([P, 2, P, 2], BF16, "hrow%d" % e) for e in range(E - 1)] + [at(2048 - 512, [P, 2, P, 2], BF16, "hrow3")]
        ctok = [sbuf([P, T], F32, "ctok%d" % u) for u in range(2)]

        def layer1_gather(e):
            xgw.append(sbuf([P, C], U32, "xgw%d" % e, tag="xgw%d" % (e % 3)))
            nc.vector.tensor_copy(xgw[e][:], xw[:].bitcast(U32).indirect(list1[:, entries(e)]))
            nc.vector.tensor_copy(xgs[:, slots(e)], xs[:].indirect(list1[:, entries(e)]))

        def layer1_product(e, first, width, tag):
            bank = psum.tile([P, width], F32, name="h_bank", tag=tag)
            nc.tensor.matmul_mx(
                out=bank[:],
                lhsT=xgw[e][:].bitcast(FP8X4),
                lhsT_scale=xgs[:, slots(e)],
                rhs=w1w[e][:, 2 * first : 2 * (first + width)].bitcast(FP4X4),
                rhs_scale=w1s[:, e, first : first + width],
                start=True,
                stop=True,
            )
            return hrow[e][:, :, first // 4 : (first + width) // 4, :], bank[:].rearrange("s (p u d) -> s u p d", u=2, d=2)

        def gate_on_scalar(e, rows, sums):
            nc.scalar.activation(out=rows, in_=sums, func=COPY, scale=g1[:, e : e + 1])

        def gate_on_vector(e, rows, sums):
            nc.vector.tensor_scalar(out=rows, in0=sums, scalar1=g1[:, e : e + 1], scalar2=None, op0=MULT)

        def turn(pieces, letter):
            bank = psum.tile([P, len(pieces) * C], F32, name="turn_bank", tag=letter)
            for j, (e, u) in enumerate(pieces):
                words = hrow[e][:].rearrange("s u p d -> s (u p d)").bitcast(F32)
                nc.tensor.transpose(bank[:, slots(j)], words[:, u * P : (u + 1) * P], ident[:])
            return bank

        def turned(pieces, letter, copy):
            held = sbuf([P, len(pieces) * C], F32, "turned%d%d" % pieces[0])
            copy(held[:], turn(pieces, letter)[:])
            return held

        layer1_gather(0)
        high = layer1_product(0, H // 2, H // 2, "b")
        quarters = [layer1_product(0, j * H // 4, H // 4, "ad"[j]) for j in range(2)]
        layer1_gather(1)
        gate_on_scalar(0, *high)
        for quarter in quarters:
            gate_on_vector(0, *quarter)
        zero0 = turned([(0, 0)], "f", nc.vector.tensor_copy)
        zero1 = turned([(0, 1)], "h", nc.scalar.copy)
        gate_on_scalar(1, *layer1_product(1, 0, H, "c"))
        one0 = turned([(1, 0)], "g", nc.scalar.copy)
        late_sums = {}
        for e in range(2, E):
            layer1_gather(e)
            late_sums[e] = layer1_product(e, 0, H, ("b", "a")[e - 2])
            gate_on_scalar(e, late_sums[e][0][:, 0], late_sums[e][1][:, 0])
        last0 = turned([(2, 0), (3, 0)], "d", nc.scalar.copy)
        for e in range(2, E):
            gate_on_scalar(e, late_sums[e][0][:, 1], late_sums[e][1][:, 1])
        late1 = turned([(1, 1), (2, 1), (3, 1)], "e", nc.scalar.copy)
        half = LIST_COLS // 2
        for u, first, last, words in (
            (0, 0, LIST_COLS, zero0[:]),
            (1, 0, half, zero1[:, 0 : C // 2]),
            (0, LIST_COLS, 2 * LIST_COLS, one0[:]),
            (1, half, LIST_COLS, zero1[:, C // 2 : C]),
            (0, 2 * LIST_COLS, 4 * LIST_COLS, last0[:]),
            (1, LIST_COLS, 4 * LIST_COLS, late1[:]),
        ):
            nc.vector.tensor_copy(ctok[u][:].indirect(list1[:, first:last]), words)

        def gpsimd_round(rounded, values):
            nc.gpsimd.tensor_scalar(out=rounded, in0=values, scalar1=1.0, scalar2=0.0, op0=MULT, op1=ADD)

        def scalar_round(rounded, values):
            nc.scalar.copy(rounded.rearrange("p (c i) t -> p c t i", i=4), values.rearrange("p t (c i) -> p c t i", i=4))

        w2b = [sbuf([P, N, 4], BF16, "w2b0"), at(0, [P, N, 4], BF16, "w2b1"), sbuf([P, N, 4], BF16, "w2b2"), at(2048, [P, N, 4], BF16, "w2b3")]
        for f, first, last in ((0, 0, N), (2, 0, N), (3, N // 2, N)):
            gpsimd_round(w2b[f][:, first:last], w2raw[f][:, :, first:last].rearrange("p t n -> p n t"))
        for f, first, last in ((1, 0, N), (3, 0, N // 2)):
            scalar_round(w2b[f][:, first:last], w2raw[f][:, :, first:last])
        cplane = [sbuf([P, T], BF16, "cplane%d" % d) for d in range(2)]
        pairs = ctok[0][:].bitcast(BF16).rearrange("p (s d) -> p s d", d=2)
        for d in range(2):
            nc.scalar.copy(cplane[d][:], pairs[:, :, d])

        cpair = [at((6208, 9216, 7232, 5184)[f], [P, 2, C, 2], BF16, "cpair%d" % f) for f in range(E)]
        cgmid = sbuf([P, 2 * C, 4], BF16, "cgmid", tag="cplane0")
        cg = [sbuf([P, C, 4], BF16, "cg0")[:], cgmid[:, slots(0), :], cgmid[:, slots(1), :], sbuf([P, C, 4], BF16, "cg3")[:]]
        w2s = sbuf([P, E, N], U8, "w2s")
        cs = sbuf([P, T], U8, "cs")
        otok = [sbuf([P, T], F32, "otok%d" % v) for v in range(2)]
        w2w = {}

        def gather_values(f, d):
            nc.scalar.activation(out=cpair[f][:, 0, :, d], in_=cplane[d][:].indirect(list2[:, entries(f)]), func=COPY)

        def gather_pairs(f, u):
            words = cpair[f][:, u].rearrange("p s d -> p (s d)").bitcast(U32)
            nc.vector.tensor_copy(words, ctok[u][:].bitcast(U32).indirect(list2[:, entries(f)]))

        def weave(f):
            nc.scalar.copy(
                cg[f].rearrange("p s t -> p (s t)").bitcast(F32).rearrange("p (s u) -> p s u", u=2),
                cpair[f][:].rearrange("p u s d -> p (u s d)").bitcast(F32).rearrange("p (u s) -> p s u", u=2),
            )

        def w2_quantise(f, codes):
            w2w[f] = codes
            nc.vector.quantize_mx(out=w2w[f][:].bitcast(FP8X4), scales=w2s[:, f, :], in_=w2b[f][:].rearrange("p n t -> p (n t)"))

        def c_quantise(first, values):
            count = values.shape[1] // C
            codes = sbuf([P, count * C], U32, "cw%d" % first)
            nc.vector.quantize_mx(out=codes[:].bitcast(FP8X4), scales=cs[:, span(first, count)], in_=values.rearrange("p s t -> p (s t)"))
            return codes

        def layer2_products(first, count, v, codes, letter):
            sums = psum.tile([P, count * C], F32, name="y_bank", tag=letter)
            for j in range(count):
                nc.tensor.matmul_mx(
                    out=sums[:, slots(j)],
                    lhsT=w2w[first + j][:, v * P : (v + 1) * P].bitcast(FP8X4),
                    lhsT_scale=w2s[:, first + j, v * P : (v + 1) * P],
                    rhs=codes[:, slots(j)].bitcast(FP8X4),
                    rhs_scale=cs[:, slots(first + j)],
                    start=True,
                    stop=True,
                )
            return sums

        def gate_sums(first, count, v, sums):
            gated = sbuf([P, count * C], F32, "gated%d%d" % (first, v))
            nc.vector.tensor_tensor(gated[:], sums[:], g2[:, span(first, count)], MULT)
            return gated

        def window(first, count, v):
            return otok[v][:].indirect(list2[:, list_span(first, count)])

        def scalar_scatter(first, count, v, gated):
            nc.scalar.activation(out=window(first, count, v), in_=gated[:], func=COPY)

        w2_quantise(0, sbuf([P, N], U32, "w2w0", tag="w2raw1"))
        for d in range(2):
            for f in range(2):
                gather_values(f, d)
        gather_values(3, 0)
        for f, u in ((0, 1), (1, 1), (2, 0), (2, 1)):
            gather_pairs(f, u)
        for f in range(E - 1):
            weave(f)
        gather_values(3, 1)
        codes = c_quantise(0, cg[0])
        first_sums = [layer2_products(0, 1, v, codes, "ab"[v]) for v in range(2)]
        gather_pairs(3, 1)
        weave(3)
        for f in (1, 2):
            w2_quantise(f, at((8192 + 64, 10240 - 64)[f - 1], [P, N], U32, "w2w%d" % f))
        codes = c_quantise(1, cgmid[:])
        middle_sums = [layer2_products(1, 2, v, codes, "cd"[v]) for v in range(2)]
        for v in range(2):
            scalar_scatter(0, 1, v, gate_sums(0, 1, v, first_sums[v]))
        w2_quantise(3, at(4096 + 128, [P, N], U32, "w2w3"))
        codes = c_quantise(3, cg[3])
        last_sums = [layer2_products(3, 1, v, codes, "ef"[v]) for v in range(2)]
        middle_gated = [gate_sums(1, 2, v, middle_sums[v]) for v in range(2)]
        nc.vector.tensor_copy(window(1, 2, 0), middle_gated[0][:])
        last_held = sbuf([P, C], F32, "last_held")
        nc.scalar.copy(last_held[:], last_sums[0][:])
        scalar_scatter(1, 2, 1, middle_gated[1])
        scalar_scatter(3, 1, 1, gate_sums(3, 1, 1, last_sums[1]))
        nc.vector.tensor_tensor(window(3, 1, 0), last_held[:], g2[:, slots(3)], MULT)
        for v in range(2):
            nc.sync.dma_start(out[v * P : (v + 1) * P, :], otok[v][:])
